import numpy as np
import ml_dtypes


def mxq(x, axis, fmt="e4m3"):
    dtype, down = {"e4m3": (ml_dtypes.float8_e4m3fn, 7), "e5m2": (ml_dtypes.float8_e5m2, 14)}[fmt]
    v = np.moveaxis(np.asarray(x, np.float32).astype(ml_dtypes.bfloat16).astype(np.float64), axis, -1)
    blocks = v.reshape(v.shape[:-1] + (-1, 32))
    amax = np.abs(blocks).max(-1, keepdims=True)
    byte = np.maximum(np.where(amax > 0, np.frexp(amax)[1] - 1 + 127, 0) - down, 1)
    scale = np.exp2(byte - 127.0)
    codes = (blocks / scale).astype(np.float32).astype(dtype).astype(np.float64)
    return np.moveaxis((codes * scale).reshape(v.shape), -1, axis)


WIDE = False


def mx_kscale(k):
    if not WIDE:
        return np.ones(k)
    levels = np.array([10, -10, 5, -5, 0])
    if k % 512:
        return np.exp2(np.random.permutation(np.resize(levels, k // 32))).repeat(32)
    a = np.empty((k // 512, 16))
    for p in range(k // 512):
        a[p, :8] = np.random.permutation(np.resize(levels, 8))
        for g in range(8):
            far = levels[np.abs(levels - a[p, g]) >= 10]
            a[p, g + 8] = far[np.random.randint(len(far))]
    return np.exp2(a.ravel()).repeat(32)


def f64(x):
    return np.asarray(x).astype(np.float64)


def striped(idx):
    return np.tile(idx.reshape(-1, 16).T, (8, 1)).astype(np.uint16)


def unstriped(offs):
    return offs[:16].T.reshape(-1).astype(np.int64)


E2M1 = np.array([0.0, 0.5, 1.0, 1.5, 2.0, 3.0, 4.0, 6.0, -0.0, -0.5, -1.0, -1.5, -2.0, -3.0, -4.0, -6.0])


def pack_weight(w, fmt):
    k, n = w.shape
    w = f64(np.asarray(w, np.float32).astype(ml_dtypes.bfloat16)).reshape(k // 32, 32, n)
    amax = np.abs(w).max(1)
    if fmt == "e4m3":
        byte = np.frexp(amax)[1] - 1 + 127 - 7
    else:
        mant, ex = np.frexp(amax / 6.0)
        byte = np.where(mant > 0.5, ex, ex - 1) + 127
    byte = np.clip(np.where(amax > 0, byte, 1), 1, 254)
    scaled = (w * np.exp2(127.0 - byte)[:, None, :]).reshape(k, n).astype(np.float32)
    by_word = np.ascontiguousarray(scaled.reshape(k // 512, 128, 4, n).transpose(0, 1, 3, 2))
    if fmt == "e4m3":
        words = by_word.astype(ml_dtypes.float8_e4m3fn).view(np.uint8)
    else:
        c = by_word.astype(ml_dtypes.float4_e2m1fn).view(np.uint8) & 0xF
        words = (c[..., 0::2] | (c[..., 1::2] << 4)).reshape(k // 512, 128, 2 * n)
    return np.ascontiguousarray(words), np.ascontiguousarray(byte.astype(np.uint8).reshape(k // 512, 16, n))


def unpack_weight(words, scales, fmt):
    g, _, n = scales.shape
    words = np.ascontiguousarray(words).reshape(g, 128, n, -1)
    if fmt == "e4m3":
        vals = words.view(ml_dtypes.float8_e4m3fn).astype(np.float64)
    else:
        nib = np.empty((g, 128, n, 4), np.uint8)
        nib[..., 0::2] = words & 0xF
        nib[..., 1::2] = words >> 4
        vals = E2M1[nib]
    vals = vals * np.repeat(np.exp2(scales.astype(np.float64) - 127.0), 8, axis=1)[..., None]
    return vals.transpose(0, 1, 3, 2).reshape(g * 512, n)


def gelu(v):
    return 0.5 * v * (1.0 + np.tanh(np.sqrt(2.0 / np.pi) * (v + 0.044715 * v**3)))


def bf(x):
    return np.asarray(x, np.float32).astype(ml_dtypes.bfloat16)


def planes(Y):
    n, m = Y.shape
    b = f64(bf(Y)).reshape(n // 32, 32, m)
    amax = np.abs(b).max(1)
    byte = np.clip(np.where(amax > 0, np.frexp(amax)[1] - 1 + 127 - 7, 1), 1, 254)
    codes = (b * np.exp2(127.0 - byte)[:, None, :]).reshape(n, m).astype(np.float32).astype(ml_dtypes.float8_e4m3fn).view(np.uint8)
    words = codes.reshape(n // 512, 128, 4, m).transpose(0, 1, 3, 2)
    return np.ascontiguousarray(words), np.ascontiguousarray(byte.astype(np.uint8).reshape(n // 512, 16, m))


K, H, N, T, S, P = 1024, 1024, 512, 4096, 1024, 512

def setup_inputs():
    n = np.random.standard_normal
    s = mx_kscale(K)[:, None]
    u = mx_kscale(H)[:, None]
    d = {}
    d["tab_words"], d["tab_scales"] = pack_weight(n((K, T)) * s, "e2m1")
    d["offs"] = striped(np.random.permutation(T)[:S])
    d["pos1"] = striped(np.random.permutation(S)[:P])
    d["pos2"] = striped(np.random.permutation(S)[:P])
    d["w1"] = (1.2 * n((K, H)) / s / np.sqrt(K)).astype(np.float32)
    d["w2_words"], d["w2_scales"] = pack_weight(1.2 * n((K, H)) / s / np.sqrt(K), "e4m3")
    d["gain"] = (np.exp(0.3 * n(H)) * u[:, 0]).astype(np.float32)
    d["w3_words"], d["w3_scales"] = pack_weight(n((H, N)) / u * np.exp(0.8 * n(N)) / np.sqrt(H), "e2m1")
    return d

def reference(tab_words, tab_scales, offs, pos1, pos2, w1, w2_words, w2_scales, gain, w3_words, w3_scales):
    v = unpack_weight(tab_words, tab_scales, "e2m1")[:, unstriped(offs)]
    w1q = mxq(f64(w1), 0, "e4m3")
    w2 = unpack_weight(w2_words, w2_scales, "e4m3")
    w3 = unpack_weight(w3_words, w3_scales, "e2m1")
    behind = w1q.T @ v
    ahead = w2.T @ v
    diff = behind[:, unstriped(pos1)] - ahead[:, unstriped(pos2)]
    h = f64(gain)[:, None] * np.log(1.0 + np.square(diff))
    y = w3.T @ mxq(h, 0, "e4m3")
    words, scales = planes(y)
    return y, words, scales

@@ -1,0 +1,288 @@
+from contextlib import ExitStack
+
+import concourse.mybir as mybir
+
+K, H, N, T, S, J = 1024, 1024, 512, 4096, 1024, 512
+P = 128
+FLOPS = 2 * (2 * K * H * S + H * N * J)
+
+F32 = mybir.dt.float32
+BF16 = mybir.dt.bfloat16
+I32 = mybir.dt.int32
+U32 = mybir.dt.uint32
+U16 = mybir.dt.uint16
+U8 = mybir.dt.uint8
+FP8X4 = mybir.dt.float8_e4m3fn_x4
+FP4X4 = mybir.dt.float4_e2m1fn_x4
+ACT = mybir.ActivationFunctionType
+ALU = mybir.AluOpType
+
+V_CASTS = ((0, 0),)
+
+
+def tile_list_ring_contrast_forecast_kernel(
+    tc, tab_words, tab_scales, offs, pos1, pos2, w1, w2_words, w2_scales, gain, w3_words, w3_scales,
+    out_0, out_1, out_2,
+):
+    nc = tc.nc
+    with ExitStack() as ctx:
+        lists = ctx.enter_context(tc.tile_pool(name="lists", bufs=1))
+        keep = ctx.enter_context(tc.tile_pool(name="keep", bufs=1))
+        ring = ctx.enter_context(tc.tile_pool(name="ring", bufs=3))
+        windows = ctx.enter_context(tc.tile_pool(name="windows", bufs=6))
+        psum = ctx.enter_context(tc.psum_pool(name="psum", bufs=8))
+
+        def held(shape, dtype, name, tag=None):
+            return keep.tile(shape, dtype, name=name, tag=tag or name, align_bytes=64)
+
+        offs_t = lists.tile([P, S // 16], U16, name="offs_t")
+        pos1_t = lists.tile([P, J // 16], U16, name="pos1_t")
+        pos2_t = lists.tile([P, J // 16], U16, name="pos2_t")
+        gain_t = held([P, 2, 4], F32, "gain_t")
+
+        tab_s = held([P, T], U8, "tab_s", "first")
+        for q in range(4):
+            nc.vector.memset(tab_s[32 * q : 32 * q + 24, :].bitcast(I32), 0)
+        w_s_raw = held([P, 2 * H], U8, "w_s_raw")
+        nc.vector.memset(w_s_raw[:].bitcast(I32), 0)
+        v_s = [held([P, S], U8, f"v_s{a}") for a in range(2)]
+        for a in range(2):
+            nc.vector.memset(v_s[a][:].bitcast(I32), 0)
+        warm_in = held([P, 2], F32, "warm_in")
+        nc.gpsimd.memset(warm_in[:], 1.0)
+        warm = held([P, 2], F32, "warm")
+        nc.scalar.activation(warm[:], warm_in[:], ACT.Ln)
+
+        nc.sync.dma_start(offs_t[:], offs)
+        for q in range(4):
+            nc.sync.dma_start(
+                tab_s[32 * q + 24 : 32 * q + 32, :].bitcast(I32), tab_scales[:, 4 * q : 4 * q + 4, :].bitcast(I32)
+            )
+        tab_w = [held([P, T], U16, f"tab_w{a}") for a in range(2)]
+        nc.sync.dma_start(tab_w[0][:].bitcast(I32), tab_words[0].bitcast(I32))
+        nc.sync.dma_start(pos2_t[:], pos2)
+        nc.sync.dma_start(pos1_t[:], pos1)
+        w2_raw = [held([P, 2, 512], I32, f"w2_raw{b}") for b in range(2)]
+        w2_src = w2_words.rearrange("a p c i -> p a (c i)").bitcast(I32)
+        nc.sync.dma_start(w2_raw[0][:], w2_src[:, :, 0:512])
+        nc.sync.dma_start(tab_w[1][:].bitcast(I32), tab_words[1].bitcast(I32))
+        nc.sync.dma_start(w2_raw[1][:], w2_src[:, :, 512:1024])
+        for q in range(4):
+            nc.scalar.dma_start(
+                w_s_raw[32 * q : 32 * q + 4, :].bitcast(I32).rearrange("r (a c) -> r a c", a=2),
+                w2_scales[:, 4 * q : 4 * q + 4, :].bitcast(I32).rearrange("a r c -> r a c"),
+            )
+        nc.gpsimd.dma_start(gain_t[:], gain.rearrange("(b p t) -> p b t", b=2, t=4))
+
+        v_s_top = held([P, S], U8, "v_s_top")
+        nc.vector.tensor_copy(v_s_top[:], tab_s[:].indirect(offs_t[:]))
+        for a in range(2):
+            nc.scalar.dma_start(v_s[a][0:100, :].bitcast(I32), v_s_top[24 + 4 * a : 124 + 4 * a, :].bitcast(I32))
+        w1_raw = {}
+
+        def load_w1(a, b, tag):
+            w1_raw[a, b] = held([P, 4, 512], F32, f"w1_raw{a}{b}", tag)
+            nc.sync.dma_start(
+                w1_raw[a, b][:],
+                w1[512 * a : 512 * (a + 1), 512 * b : 512 * (b + 1)].rearrange("(p j) c -> p j c", j=4),
+            )
+
+        load_w1(0, 0, "first")
+        v_w = [[held([P, 512], U16, f"v_w{a}{h}") for h in range(2)] for a in range(2)]
+
+        def gather_words(a, h):
+            nc.vector.tensor_copy(v_w[a][h][:], tab_w[a][:].indirect(offs_t[:, 32 * h : 32 * (h + 1)]))
+
+        def deal_bytes(dst, src):
+            nc.vector.tensor_copy(
+                dst.rearrange("p a (t u i) -> p a u t i", t=4, i=16),
+                src.rearrange("p a (u i t) -> p a u t i", t=4, i=16),
+            )
+
+        w2_s = [held([P, 2, 512], U8, f"w2_s{b}") for b in range(2)]
+        w2_c = [held([P, 2, 512], I32, f"w2_c{b}") for b in range(2)]
+
+        def deal_w2_scales(b):
+            deal_bytes(w2_s[b][:], w_s_raw[:].rearrange("p (a c) -> p a c", a=2)[:, :, 512 * b : 512 * (b + 1)])
+
+        def deal_w2(b):
+            nc.vector.tensor_copy(
+                w2_c[b][:].rearrange("p a (t u i) -> p a u t i", t=4, i=4),
+                w2_raw[b][:].rearrange("p a (u i t) -> p a u t i", t=4, i=4),
+            )
+
+        gather_words(0, 0)
+        deal_w2_scales(0)
+        deal_w2(0)
+        gather_words(1, 0)
+        gather_words(0, 1)
+        load_w1(1, 0, "tab_w0")
+        gather_words(1, 1)
+        load_w1(0, 1, "tab_w1")
+        deal_w2_scales(1)
+        deal_w2(1)
+        load_w1(1, 1, "w2_raw1")
+        w3_raw = held([P, 2, N], U16, "w3_raw", "v_s_top")
+        nc.sync.dma_start(w3_raw[:].bitcast(I32), w3_words.bitcast(I32).rearrange("a p c -> p a c"))
+        for q in range(4):
+            nc.sync.dma_start(
+                w_s_raw[32 * q : 32 * q + 4, 0 : 2 * N].bitcast(I32).rearrange("r (a c) -> r a c", a=2),
+                w3_scales[:, 4 * q : 4 * q + 4, :].bitcast(I32).rearrange("a r c -> r a c"),
+            )
+
+        w1_c = {}
+        w1_s = {}
+        w1_g = {}
+
+        def cast_w1(a, b):
+            g = held([P, 4 * 512], BF16, f"w1_g{a}{b}")
+            w1_g[a, b] = g
+            dst = g[:].rearrange("p (t m j) -> p m t j", t=4, j=4)
+            src = w1_raw[a, b][:].rearrange("p j (m t) -> p m t j", t=4)
+            if (a, b) in V_CASTS:
+                nc.vector.tensor_copy(dst, src)
+            else:
+                for u in range(2):
+                    nc.scalar.copy(dst[:, 64 * u : 64 * (u + 1)], src[:, 64 * u : 64 * (u + 1)])
+
+        def quant_w1(a, b):
+            w1_c[a, b] = held([P, 512], U32, f"w1_c{a}{b}")
+            w1_s[a, b] = held([P, 512], U8, f"w1_s{a}{b}")
+            nc.vector.quantize_mx(out=w1_c[a, b][:].bitcast(FP8X4), scales=w1_s[a, b][:], in_=w1_g[a, b][:])
+
+        def first_half(window, h, codes, scales):
+            acc = psum.tile([P, 512], F32, name="acc")
+            for a in range(2):
+                nc.tensor.matmul_mx(
+                    out=acc[:], lhsT=codes(a).bitcast(FP8X4), lhsT_scale=scales(a),
+                    rhs=v_w[a][h][:].bitcast(FP4X4), rhs_scale=v_s[a][:, 512 * h : 512 * (h + 1)],
+                    start=(a == 0), stop=(a == 1),
+                )
+            nc.scalar.copy(window[:, 512 * h : 512 * (h + 1)], acc[:])
+
+        ahead = {}
+        ahead_all = {}
+
+        def ahead_half(b, t, h):
+            if h == 0:
+                ahead_all[b, t] = windows.tile([P, S], F32, name="window", align_bytes=64)
+            cols = slice(128 * t, 128 * (t + 1))
+            first_half(ahead_all[b, t], h, lambda a: w2_c[b][:, a, cols], lambda a: w2_s[b][:, a, cols])
+            if h == 1:
+                ahead[b, t] = held([P, J], F32, f"ahead{b}{t}")
+                nc.vector.tensor_copy(ahead[b, t][:], ahead_all[b, t][:].indirect(pos2_t[:]))
+
+        logs = [held([P, 4, J], F32, f"logs{b}") for b in range(2)]
+
+        def behind_all(b, t):
+            window = windows.tile([P, S], F32, name="window", align_bytes=64)
+            cols = slice(128 * t, 128 * (t + 1))
+            for h in range(2):
+                first_half(window, h, lambda a: w1_c[a, b][:, cols], lambda a: w1_s[a, b][:, cols])
+            return window
+
+        def contrast(window, b, t, c0, c1):
+            diff = ring.tile([P, c1 - c0], F32, name="diff", align_bytes=64)
+            nc.vector.tensor_tensor(
+                diff[:], window[:].indirect(pos1_t[:, c0 // 16 : c1 // 16]), ahead[b, t][:, c0:c1], ALU.subtract
+            )
+            sq = ring.tile([P, c1 - c0], F32, name="sq", align_bytes=64)
+            nc.scalar.activation(sq[:], diff[:], ACT.Square)
+            nc.scalar.activation(logs[b][:, t, c0:c1], sq[:], ACT.Ln, bias=1.0)
+
+        def do_behind(b, t):
+            contrast(behind_all(b, t), b, t, 0, J)
+
+        h_c = [held([P, J], U32, f"h_c{b}") for b in range(2)]
+        h_s = [held([P, J], U8, f"h_s{b}") for b in range(2)]
+        h_g = [held([P, 4 * J], BF16, f"h_g{b}") for b in range(2)]
+
+        def gain_h(b, c0, c1):
+            nc.vector.tensor_tensor(
+                h_g[b][:, 4 * c0 : 4 * c1].rearrange("p (u i t) -> p u t i", t=4, i=4),
+                logs[b][:, :, c0:c1].rearrange("p t (u i) -> p u t i", i=4),
+                gain_t[:, b : b + 1, :].unsqueeze(3).to_broadcast([P, (c1 - c0) // 4, 4, 4]),
+                ALU.mult,
+            )
+
+        def quant_h(b, c0, c1):
+            nc.vector.quantize_mx(
+                out=h_c[b][:, c0:c1].bitcast(FP8X4), scales=h_s[b][:, c0:c1], in_=h_g[b][:, 4 * c0 : 4 * c1]
+            )
+
+        casts = [(0, 0), (1, 0), (0, 1), (1, 1)]
+        for h in range(2):
+            for t in range(4):
+                ahead_half(0, t, h)
+        for t in range(4):
+            cast_w1(*casts[t])
+            for h in range(2):
+                ahead_half(1, t, h)
+            quant_w1(*casts[t])
+
+        w3_s = held([P, 2, N], U8, "w3_s")
+        w3_c = held([P, 2, N], U16, "w3_c")
+        for t in range(4):
+            do_behind(0, t)
+        deal_bytes(w3_s[:], w_s_raw[:, 0 : 2 * N].rearrange("p (a c) -> p a c", a=2))
+        nc.vector.tensor_copy(
+            w3_c[:].rearrange("p a (t u i) -> p a u t i", t=4, i=8),
+            w3_raw[:].rearrange("p a (u i t) -> p a u t i", t=4, i=8),
+        )
+        do_behind(1, 0)
+        gain_h(0, 0, J)
+        do_behind(1, 1)
+        quant_h(0, 0, J)
+        do_behind(1, 2)
+        last = behind_all(1, 3)
+
+        y = held([P, 4, J], F32, "y")
+        y_g = held([P, 4 * J], BF16, "y_g")
+        y_c = held([P, J], U32, "y_c")
+        y_s = held([P, J], U8, "y_s")
+        out_rows = out_0.rearrange("(p t) j -> p t j", t=4)
+        out_words = out_1[0].rearrange("p m i -> p (m i)").bitcast(I32)
+
+        def third(c):
+            cols = slice(128 * c, 128 * (c + 1))
+            acc = psum.tile([P, 512], F32, name="acc")
+            for t in range(4):
+                for b in range(2):
+                    nc.tensor.matmul_mx(
+                        out=acc[:, 128 * t : 128 * (t + 1)],
+                        lhsT=w3_c[:, b, 128 * t : 128 * (t + 1)].bitcast(FP4X4),
+                        lhsT_scale=w3_s[:, b, 128 * t : 128 * (t + 1)],
+                        rhs=h_c[b][:, cols].bitcast(FP8X4), rhs_scale=h_s[b][:, cols],
+                        start=(b == 0), stop=(b == 1),
+                    )
+            nc.scalar.copy(y[:, :, cols], acc[:].rearrange("p (t j) -> p t j", t=4))
+            nc.sync.dma_start(out_rows[:, :, cols], y[:, :, cols])
+
+        def round_y(c):
+            nc.vector.tensor_copy(
+                y_g[:, 512 * c : 512 * (c + 1)].rearrange("p (u i t) -> p u t i", t=4, i=4),
+                y[:, :, 128 * c : 128 * (c + 1)].rearrange("p t (u i) -> p u t i", i=4),
+            )
+
+        def quant_y(c):
+            cols = slice(128 * c, 128 * (c + 1))
+            nc.vector.quantize_mx(
+                out=y_c[:, cols].bitcast(FP8X4), scales=y_s[:, cols], in_=y_g[:, 512 * c : 512 * (c + 1)]
+            )
+
+        for step in range(9):
+            if step < 4:
+                contrast(last, 1, 3, 128 * step, 128 * (step + 1))
+            if 0 <= step - 3 < 4:
+                quant_h(1, 128 * (step - 3), 128 * (step - 2))
+                third(step - 3)
+            if 0 <= step - 2 < 4:
+                gain_h(1, 128 * (step - 2), 128 * (step - 1))
+            if 0 <= step - 5 < 4:
+                quant_y(step - 5)
+            if 0 <= step - 4 < 4:
+                round_y(step - 4)
+        nc.sync.dma_start(out_words, y_c[:].bitcast(I32))
+        for q in range(4):
+            eng = nc.scalar if q % 2 else nc.sync
+            eng.dma_start(out_2[0, 4 * q : 4 * q + 4, :].bitcast(I32), y_s[32 * q : 32 * q + 4, :].bitcast(I32))

@@ -17,7 +17,7 @@ FP4X4 = mybir.dt.float4_e2m1fn_x4
 ACT = mybir.ActivationFunctionType
 ALU = mybir.AluOpType
 
-V_CASTS = ((0, 0),)
+CASTS = {(0, 0): "g", (1, 0): "g", (0, 1): "g", (1, 1): "g"}
 
 
 def tile_list_ring_contrast_forecast_kernel(
@@ -29,7 +29,6 @@ def tile_list_ring_contrast_forecast_kernel(
         lists = ctx.enter_context(tc.tile_pool(name="lists", bufs=1))
         keep = ctx.enter_context(tc.tile_pool(name="keep", bufs=1))
         ring = ctx.enter_context(tc.tile_pool(name="ring", bufs=3))
-        windows = ctx.enter_context(tc.tile_pool(name="windows", bufs=6))
         psum = ctx.enter_context(tc.psum_pool(name="psum", bufs=8))
 
         def held(shape, dtype, name, tag=None):
@@ -38,46 +37,49 @@ def tile_list_ring_contrast_forecast_kernel(
         offs_t = lists.tile([P, S // 16], U16, name="offs_t")
         pos1_t = lists.tile([P, J // 16], U16, name="pos1_t")
         pos2_t = lists.tile([P, J // 16], U16, name="pos2_t")
-        gain_t = held([P, 2, 4], F32, "gain_t")
 
-        tab_s = held([P, T], U8, "tab_s", "first")
-        for q in range(4):
-            nc.vector.memset(tab_s[32 * q : 32 * q + 24, :].bitcast(I32), 0)
-        w_s_raw = held([P, 2 * H], U8, "w_s_raw")
-        nc.vector.memset(w_s_raw[:].bitcast(I32), 0)
-        v_s = [held([P, S], U8, f"v_s{a}") for a in range(2)]
-        for a in range(2):
-            nc.vector.memset(v_s[a][:].bitcast(I32), 0)
+        tab_s = held([P, T], U8, "tab_s")
+        w_s_raw = held([P, H], U8, "w_s_raw")
+        planes = held([P, 2, S + H], U8, "planes")
+        nc.vector.memset(w_s_raw[0:96, :].bitcast(I32), 0)
+        nc.vector.memset(tab_s[0:96, :].bitcast(I32), 0)
+        nc.gpsimd.memset(planes[:].bitcast(I32), 0)
         warm_in = held([P, 2], F32, "warm_in")
         nc.gpsimd.memset(warm_in[:], 1.0)
         warm = held([P, 2], F32, "warm")
         nc.scalar.activation(warm[:], warm_in[:], ACT.Ln)
 
         nc.sync.dma_start(offs_t[:], offs)
-        for q in range(4):
-            nc.sync.dma_start(
-                tab_s[32 * q + 24 : 32 * q + 32, :].bitcast(I32), tab_scales[:, 4 * q : 4 * q + 4, :].bitcast(I32)
-            )
+        nc.sync.dma_start(w_s_raw[96:128, :].bitcast(I32), w2_scales.bitcast(I32).rearrange("a q c -> q a c"))
+        nc.sync.dma_start(tab_s[96:128, :].bitcast(I32), tab_scales.bitcast(I32).rearrange("a q c -> q a c"))
         tab_w = [held([P, T], U16, f"tab_w{a}") for a in range(2)]
         nc.sync.dma_start(tab_w[0][:].bitcast(I32), tab_words[0].bitcast(I32))
-        nc.sync.dma_start(pos2_t[:], pos2)
-        nc.sync.dma_start(pos1_t[:], pos1)
-        w2_raw = [held([P, 2, 512], I32, f"w2_raw{b}") for b in range(2)]
+        w2_raw = [held([P, 2, 512], I32, "w2_raw0")]
         w2_src = w2_words.rearrange("a p c i -> p a (c i)").bitcast(I32)
         nc.sync.dma_start(w2_raw[0][:], w2_src[:, :, 0:512])
+        nc.sync.dma_start(pos2_t[:], pos2)
+        nc.sync.dma_start(pos1_t[:], pos1)
         nc.sync.dma_start(tab_w[1][:].bitcast(I32), tab_words[1].bitcast(I32))
-        nc.sync.dma_start(w2_raw[1][:], w2_src[:, :, 512:1024])
+
+        def deal_bytes(dst, src):
+            nc.vector.tensor_copy(
+                dst.rearrange("p (b t u i) -> p b u t i", t=4, u=8, i=16),
+                src.rearrange("p (b u i t) -> p b u t i", t=4, u=8, i=16),
+            )
+
+        rows = held([P, S + H], U8, "rows")
+        deal_bytes(rows[:, S : S + H], w_s_raw[:])
+        v_s_rows = held([P, S], U8, "v_s_rows")
+        nc.vector.tensor_copy(v_s_rows[:], tab_s[:].indirect(offs_t[:]))
+        gain_t = held([P, 2, 4], F32, "gain_t", "tab_s")
+        nc.sync.dma_start(gain_t[:], gain.rearrange("(b p t) -> p b t", b=2, t=4))
+        nc.vector.tensor_copy(rows[:, 0:S].bitcast(I32), v_s_rows[:].bitcast(I32))
         for q in range(4):
             nc.scalar.dma_start(
-                w_s_raw[32 * q : 32 * q + 4, :].bitcast(I32).rearrange("r (a c) -> r a c", a=2),
-                w2_scales[:, 4 * q : 4 * q + 4, :].bitcast(I32).rearrange("a r c -> r a c"),
+                planes[32 * q : 32 * q + 4].bitcast(I32), rows[96 + 8 * q : 104 + 8 * q, :].bitcast(I32)
             )
-        nc.gpsimd.dma_start(gain_t[:], gain.rearrange("(b p t) -> p b t", b=2, t=4))
-
-        v_s_top = held([P, S], U8, "v_s_top")
-        nc.vector.tensor_copy(v_s_top[:], tab_s[:].indirect(offs_t[:]))
-        for a in range(2):
-            nc.scalar.dma_start(v_s[a][0:100, :].bitcast(I32), v_s_top[24 + 4 * a : 124 + 4 * a, :].bitcast(I32))
+        w2_raw.append(held([P, 2, 512], I32, "w2_raw1", "rows"))
+        nc.sync.dma_start(w2_raw[1][:], w2_src[:, :, 512:1024])
         w1_raw = {}
 
         def load_w1(a, b, tag):
@@ -87,23 +89,12 @@ def tile_list_ring_contrast_forecast_kernel(
                 w1[512 * a : 512 * (a + 1), 512 * b : 512 * (b + 1)].rearrange("(p j) c -> p j c", j=4),
             )
 
-        load_w1(0, 0, "first")
         v_w = [[held([P, 512], U16, f"v_w{a}{h}") for h in range(2)] for a in range(2)]
 
         def gather_words(a, h):
             nc.vector.tensor_copy(v_w[a][h][:], tab_w[a][:].indirect(offs_t[:, 32 * h : 32 * (h + 1)]))
 
-        def deal_bytes(dst, src):
-            nc.vector.tensor_copy(
-                dst.rearrange("p a (t u i) -> p a u t i", t=4, i=16),
-                src.rearrange("p a (u i t) -> p a u t i", t=4, i=16),
-            )
-
-        w2_s = [held([P, 2, 512], U8, f"w2_s{b}") for b in range(2)]
         w2_c = [held([P, 2, 512], I32, f"w2_c{b}") for b in range(2)]
-
-        def deal_w2_scales(b):
-            deal_bytes(w2_s[b][:], w_s_raw[:].rearrange("p (a c) -> p a c", a=2)[:, :, 512 * b : 512 * (b + 1)])
 
         def deal_w2(b):
             nc.vector.tensor_copy(
@@ -112,23 +103,15 @@ def tile_list_ring_contrast_forecast_kernel(
             )
 
         gather_words(0, 0)
-        deal_w2_scales(0)
         deal_w2(0)
-        gather_words(1, 0)
+        load_w1(0, 0, "w2_raw0")
         gather_words(0, 1)
         load_w1(1, 0, "tab_w0")
+        gather_words(1, 0)
         gather_words(1, 1)
         load_w1(0, 1, "tab_w1")
-        deal_w2_scales(1)
         deal_w2(1)
-        load_w1(1, 1, "w2_raw1")
-        w3_raw = held([P, 2, N], U16, "w3_raw", "v_s_top")
-        nc.sync.dma_start(w3_raw[:].bitcast(I32), w3_words.bitcast(I32).rearrange("a p c -> p a c"))
-        for q in range(4):
-            nc.sync.dma_start(
-                w_s_raw[32 * q : 32 * q + 4, 0 : 2 * N].bitcast(I32).rearrange("r (a c) -> r a c", a=2),
-                w3_scales[:, 4 * q : 4 * q + 4, :].bitcast(I32).rearrange("a r c -> r a c"),
-            )
+        load_w1(1, 1, "rows")
 
         w1_c = {}
         w1_s = {}
@@ -139,14 +122,18 @@ def tile_list_ring_contrast_forecast_kernel(
             w1_g[a, b] = g
             dst = g[:].rearrange("p (t m j) -> p m t j", t=4, j=4)
             src = w1_raw[a, b][:].rearrange("p j (m t) -> p m t j", t=4)
-            if (a, b) in V_CASTS:
+            if CASTS[a, b] == "v":
                 nc.vector.tensor_copy(dst, src)
+            elif CASTS[a, b] == "g":
+                for u in range(4):
+                    part = slice(32 * u, 32 * (u + 1))
+                    nc.gpsimd.tensor_scalar(dst[:, part], src[:, part], 1.0, 0.0, ALU.mult, ALU.add)
             else:
                 for u in range(2):
                     nc.scalar.copy(dst[:, 64 * u : 64 * (u + 1)], src[:, 64 * u : 64 * (u + 1)])
 
-        def quant_w1(a, b):
-            w1_c[a, b] = held([P, 512], U32, f"w1_c{a}{b}")
+        def quant_w1(a, b, tag):
+            w1_c[a, b] = held([P, 512], U32, f"w1_c{a}{b}", tag)
             w1_s[a, b] = held([P, 512], U8, f"w1_s{a}{b}")
             nc.vector.quantize_mx(out=w1_c[a, b][:].bitcast(FP8X4), scales=w1_s[a, b][:], in_=w1_g[a, b][:])
 
@@ -155,7 +142,7 @@ def tile_list_ring_contrast_forecast_kernel(
             for a in range(2):
                 nc.tensor.matmul_mx(
                     out=acc[:], lhsT=codes(a).bitcast(FP8X4), lhsT_scale=scales(a),
-                    rhs=v_w[a][h][:].bitcast(FP4X4), rhs_scale=v_s[a][:, 512 * h : 512 * (h + 1)],
+                    rhs=v_w[a][h][:].bitcast(FP4X4), rhs_scale=planes[:, a, 512 * h : 512 * (h + 1)],
                     start=(a == 0), stop=(a == 1),
                 )
             nc.scalar.copy(window[:, 512 * h : 512 * (h + 1)], acc[:])
@@ -165,9 +152,9 @@ def tile_list_ring_contrast_forecast_kernel(
 
         def ahead_half(b, t, h):
             if h == 0:
-                ahead_all[b, t] = windows.tile([P, S], F32, name="window", align_bytes=64)
+                ahead_all[b, t] = held([P, S], F32, f"ahead_all{b}{t}", f"win{4 * b + t}")
             cols = slice(128 * t, 128 * (t + 1))
-            first_half(ahead_all[b, t], h, lambda a: w2_c[b][:, a, cols], lambda a: w2_s[b][:, a, cols])
+            first_half(ahead_all[b, t], h, lambda a: w2_c[b][:, a, cols], lambda a: planes[:, a, S + 512 * b + 128 * t : S + 512 * b + 128 * (t + 1)])
             if h == 1:
                 ahead[b, t] = held([P, J], F32, f"ahead{b}{t}")
                 nc.vector.tensor_copy(ahead[b, t][:], ahead_all[b, t][:].indirect(pos2_t[:]))
@@ -175,7 +162,7 @@ def tile_list_ring_contrast_forecast_kernel(
         logs = [held([P, 4, J], F32, f"logs{b}") for b in range(2)]
 
         def behind_all(b, t):
-            window = windows.tile([P, S], F32, name="window", align_bytes=64)
+            window = held([P, S], F32, f"behind_all{b}{t}", f"win{(0, 1, 2, 4)[t]}")
             cols = slice(128 * t, 128 * (t + 1))
             for h in range(2):
                 first_half(window, h, lambda a: w1_c[a, b][:, cols], lambda a: w1_s[a, b][:, cols])
@@ -214,17 +201,35 @@ def tile_list_ring_contrast_forecast_kernel(
         for h in range(2):
             for t in range(4):
                 ahead_half(0, t, h)
+        cast_w1(0, 0)
+        w3_raw = held([P, 2, N], U16, "w3_raw", "w2_raw0")
+        nc.sync.dma_start(w3_raw[:].bitcast(I32), w3_words.bitcast(I32).rearrange("a p c -> p a c"))
+        cast_w1(1, 0)
+        w3_s_raw = held([P, 2 * N], U8, "w3_s_raw", "tab_w0")
+        nc.gpsimd.memset(w3_s_raw[:].bitcast(I32), 0)
+        for q in range(4):
+            nc.sync.dma_start(
+                w3_s_raw[32 * q : 32 * q + 4, :].bitcast(I32).rearrange("r (a c) -> r a c", a=2),
+                w3_scales[:, 4 * q : 4 * q + 4, :].bitcast(I32).rearrange("a r c -> r a c"),
+            )
+        cast_w1(0, 1)
+        cast_w1(1, 1)
         for t in range(4):
-            cast_w1(*casts[t])
             for h in range(2):
                 ahead_half(1, t, h)
-            quant_w1(*casts[t])
-
+            if t == 0:
+                quant_w1(0, 0, "win3")
+            if t == 1:
+                quant_w1(1, 0, "win5")
         w3_s = held([P, 2, N], U8, "w3_s")
         w3_c = held([P, 2, N], U16, "w3_c")
-        for t in range(4):
-            do_behind(0, t)
-        deal_bytes(w3_s[:], w_s_raw[:, 0 : 2 * N].rearrange("p (a c) -> p a c", a=2))
+        do_behind(0, 0)
+        quant_w1(0, 1, "win6")
+        do_behind(0, 1)
+        quant_w1(1, 1, "win7")
+        do_behind(0, 2)
+        deal_bytes(w3_s[:].rearrange("p a c -> p (a c)"), w3_s_raw[:])
+        do_behind(0, 3)
         nc.vector.tensor_copy(
             w3_c[:].rearrange("p a (t u i) -> p a u t i", t=4, i=8),
             w3_raw[:].rearrange("p a (u i t) -> p a u t i", t=4, i=8),

@@ -17,7 +17,7 @@ FP4X4 = mybir.dt.float4_e2m1fn_x4
 ACT = mybir.ActivationFunctionType
 ALU = mybir.AluOpType
 
-CASTS = {(0, 0): "g", (1, 0): "g", (0, 1): "g", (1, 1): "g"}
+CASTS = {(0, 0): "s", (1, 0): "s", (0, 1): "v", (1, 1): "v"}
 
 
 def tile_list_ring_contrast_forecast_kernel(
@@ -28,7 +28,6 @@ def tile_list_ring_contrast_forecast_kernel(
     with ExitStack() as ctx:
         lists = ctx.enter_context(tc.tile_pool(name="lists", bufs=1))
         keep = ctx.enter_context(tc.tile_pool(name="keep", bufs=1))
-        ring = ctx.enter_context(tc.tile_pool(name="ring", bufs=3))
         psum = ctx.enter_context(tc.psum_pool(name="psum", bufs=8))
 
         def held(shape, dtype, name, tag=None):
@@ -69,14 +68,23 @@ def tile_list_ring_contrast_forecast_kernel(
 
         rows = held([P, S + H], U8, "rows")
         deal_bytes(rows[:, S : S + H], w_s_raw[:])
+        gain_t = held([P, 2, 4], F32, "gain_t", "w_s_raw")
+        nc.sync.dma_start(gain_t[:], gain.rearrange("(b p t) -> p b t", b=2, t=4))
         v_s_rows = held([P, S], U8, "v_s_rows")
         nc.vector.tensor_copy(v_s_rows[:], tab_s[:].indirect(offs_t[:]))
-        gain_t = held([P, 2, 4], F32, "gain_t", "tab_s")
-        nc.sync.dma_start(gain_t[:], gain.rearrange("(b p t) -> p b t", b=2, t=4))
+        w3_raw = held([P, 2, N], U16, "w3_raw", "tab_s")
+        nc.sync.dma_start(w3_raw[:].bitcast(I32), w3_words.bitcast(I32).rearrange("a p c -> p a c"))
         nc.vector.tensor_copy(rows[:, 0:S].bitcast(I32), v_s_rows[:].bitcast(I32))
         for q in range(4):
             nc.scalar.dma_start(
                 planes[32 * q : 32 * q + 4].bitcast(I32), rows[96 + 8 * q : 104 + 8 * q, :].bitcast(I32)
+            )
+        w3_s_raw = held([P, 2 * N], U8, "w3_s_raw", "v_s_rows")
+        nc.gpsimd.memset(w3_s_raw[:].bitcast(I32), 0)
+        for q in range(4):
+            nc.sync.dma_start(
+                w3_s_raw[32 * q : 32 * q + 4, :].bitcast(I32).rearrange("r (a c) -> r a c", a=2),
+                w3_scales[:, 4 * q : 4 * q + 4, :].bitcast(I32).rearrange("a r c -> r a c"),
             )
         w2_raw.append(held([P, 2, 512], I32, "w2_raw1", "rows"))
         nc.sync.dma_start(w2_raw[1][:], w2_src[:, :, 512:1024])
@@ -94,31 +102,37 @@ def tile_list_ring_contrast_forecast_kernel(
         def gather_words(a, h):
             nc.vector.tensor_copy(v_w[a][h][:], tab_w[a][:].indirect(offs_t[:, 32 * h : 32 * (h + 1)]))
 
-        w2_c = [held([P, 2, 512], I32, f"w2_c{b}") for b in range(2)]
+        w2_c = {}
 
-        def deal_w2(b):
+        def deal_w2(b, tag):
+            w2_c[b] = held([P, 2, 512], I32, f"w2_c{b}", tag)
             nc.vector.tensor_copy(
                 w2_c[b][:].rearrange("p a (t u i) -> p a u t i", t=4, i=4),
                 w2_raw[b][:].rearrange("p a (u i t) -> p a u t i", t=4, i=4),
             )
 
         gather_words(0, 0)
-        deal_w2(0)
+        deal_w2(0, "w2_c0")
         load_w1(0, 0, "w2_raw0")
+        gather_words(1, 0)
         gather_words(0, 1)
         load_w1(1, 0, "tab_w0")
-        gather_words(1, 0)
         gather_words(1, 1)
         load_w1(0, 1, "tab_w1")
-        deal_w2(1)
-        load_w1(1, 1, "rows")
+        w3_s = held([P, 2, N], U8, "w3_s")
+        w3_c = held([P, 2, N], U16, "w3_c")
+        deal_bytes(w3_s[:].rearrange("p a c -> p (a c)"), w3_s_raw[:])
+        nc.vector.tensor_copy(
+            w3_c[:].rearrange("p a (t u i) -> p a u t i", t=4, i=8),
+            w3_raw[:].rearrange("p a (u i t) -> p a u t i", t=4, i=8),
+        )
 
         w1_c = {}
         w1_s = {}
         w1_g = {}
 
-        def cast_w1(a, b):
-            g = held([P, 4 * 512], BF16, f"w1_g{a}{b}")
+        def cast_w1(a, b, tag=None):
+            g = held([P, 4 * 512], BF16, f"w1_g{a}{b}", tag)
             w1_g[a, b] = g
             dst = g[:].rearrange("p (t m j) -> p m t j", t=4, j=4)
             src = w1_raw[a, b][:].rearrange("p j (m t) -> p m t j", t=4)
@@ -132,8 +146,8 @@ def tile_list_ring_contrast_forecast_kernel(
                 for u in range(2):
                     nc.scalar.copy(dst[:, 64 * u : 64 * (u + 1)], src[:, 64 * u : 64 * (u + 1)])
 
-        def quant_w1(a, b, tag):
-            w1_c[a, b] = held([P, 512], U32, f"w1_c{a}{b}", tag)
+        def quant_w1(a, b):
+            w1_c[a, b] = held([P, 512], U32, f"w1_c{a}{b}")
             w1_s[a, b] = held([P, 512], U8, f"w1_s{a}{b}")
             nc.vector.quantize_mx(out=w1_c[a, b][:].bitcast(FP8X4), scales=w1_s[a, b][:], in_=w1_g[a, b][:])
 
@@ -159,26 +173,29 @@ def tile_list_ring_contrast_forecast_kernel(
                 ahead[b, t] = held([P, J], F32, f"ahead{b}{t}")
                 nc.vector.tensor_copy(ahead[b, t][:], ahead_all[b, t][:].indirect(pos2_t[:]))
 
-        logs = [held([P, 4, J], F32, f"logs{b}") for b in range(2)]
+        squares_all = [held([P, 4, J], F32, f"squares{b}") for b in range(2)]
+        squares = [[squares_all[b][:, t, :] for t in range(4)] for b in range(2)]
 
         def behind_all(b, t):
-            window = held([P, S], F32, f"behind_all{b}{t}", f"win{(0, 1, 2, 4)[t]}")
+            window = held([P, S], F32, f"behind_all{b}{t}", f"win{(1, 2, 0, 4, 6, 7, 1, 2)[4 * b + t]}")
             cols = slice(128 * t, 128 * (t + 1))
             for h in range(2):
                 first_half(window, h, lambda a: w1_c[a, b][:, cols], lambda a: w1_s[a, b][:, cols])
             return window
 
         def contrast(window, b, t, c0, c1):
-            diff = ring.tile([P, c1 - c0], F32, name="diff", align_bytes=64)
+            diff = squares[b][t][:, c0:c1]
             nc.vector.tensor_tensor(
-                diff[:], window[:].indirect(pos1_t[:, c0 // 16 : c1 // 16]), ahead[b, t][:, c0:c1], ALU.subtract
+                diff, window[:].indirect(pos1_t[:, c0 // 16 : c1 // 16]), ahead[b, t][:, c0:c1], ALU.subtract
             )
-            sq = ring.tile([P, c1 - c0], F32, name="sq", align_bytes=64)
-            nc.scalar.activation(sq[:], diff[:], ACT.Square)
-            nc.scalar.activation(logs[b][:, t, c0:c1], sq[:], ACT.Ln, bias=1.0)
+            nc.scalar.activation(diff, diff, ACT.Square)
 
-        def do_behind(b, t):
-            contrast(behind_all(b, t), b, t, 0, J)
+        logs = held([P, J, 4], F32, "logs")
+
+        def log_h(b, c0, c1):
+            nc.scalar.activation(
+                logs[:, c0:c1, :], squares_all[b][:, :, c0:c1].rearrange("p t j -> p j t"), ACT.Ln, bias=1.0
+            )
 
         h_c = [held([P, J], U32, f"h_c{b}") for b in range(2)]
         h_s = [held([P, J], U8, f"h_s{b}") for b in range(2)]
@@ -186,9 +203,9 @@ def tile_list_ring_contrast_forecast_kernel(
 
         def gain_h(b, c0, c1):
             nc.vector.tensor_tensor(
-                h_g[b][:, 4 * c0 : 4 * c1].rearrange("p (u i t) -> p u t i", t=4, i=4),
-                logs[b][:, :, c0:c1].rearrange("p t (u i) -> p u t i", i=4),
-                gain_t[:, b : b + 1, :].unsqueeze(3).to_broadcast([P, (c1 - c0) // 4, 4, 4]),
+                h_g[b][:, 4 * c0 : 4 * c1].rearrange("p (j t) -> p j t", t=4),
+                logs[:, c0:c1, :],
+                gain_t[:, b : b + 1, :].to_broadcast([P, c1 - c0, 4]),
                 ALU.mult,
             )
 
@@ -197,49 +214,45 @@ def tile_list_ring_contrast_forecast_kernel(
                 out=h_c[b][:, c0:c1].bitcast(FP8X4), scales=h_s[b][:, c0:c1], in_=h_g[b][:, 4 * c0 : 4 * c1]
             )
 
-        casts = [(0, 0), (1, 0), (0, 1), (1, 1)]
-        for h in range(2):
-            for t in range(4):
-                ahead_half(0, t, h)
+        for t, h in ((0, 0), (1, 0), (0, 1)):
+            ahead_half(0, t, h)
+        deal_w2(1, "win0")
+        load_w1(1, 1, "rows")
+        for t, h in ((1, 1), (2, 0), (2, 1)):
+            ahead_half(0, t, h)
         cast_w1(0, 0)
-        w3_raw = held([P, 2, N], U16, "w3_raw", "w2_raw0")
-        nc.sync.dma_start(w3_raw[:].bitcast(I32), w3_words.bitcast(I32).rearrange("a p c -> p a c"))
-        cast_w1(1, 0)
-        w3_s_raw = held([P, 2 * N], U8, "w3_s_raw", "tab_w0")
-        nc.gpsimd.memset(w3_s_raw[:].bitcast(I32), 0)
-        for q in range(4):
-            nc.sync.dma_start(
-                w3_s_raw[32 * q : 32 * q + 4, :].bitcast(I32).rearrange("r (a c) -> r a c", a=2),
-                w3_scales[:, 4 * q : 4 * q + 4, :].bitcast(I32).rearrange("a r c -> r a c"),
-            )
-        cast_w1(0, 1)
-        cast_w1(1, 1)
-        for t in range(4):
+        quant_w1(0, 0)
+        for b, t in ((0, 3), (1, 0)):
             for h in range(2):
-                ahead_half(1, t, h)
-            if t == 0:
-                quant_w1(0, 0, "win3")
-            if t == 1:
-                quant_w1(1, 0, "win5")
-        w3_s = held([P, 2, N], U8, "w3_s")
-        w3_c = held([P, 2, N], U16, "w3_c")
-        do_behind(0, 0)
-        quant_w1(0, 1, "win6")
-        do_behind(0, 1)
-        quant_w1(1, 1, "win7")
-        do_behind(0, 2)
-        deal_bytes(w3_s[:].rearrange("p a c -> p (a c)"), w3_s_raw[:])
-        do_behind(0, 3)
-        nc.vector.tensor_copy(
-            w3_c[:].rearrange("p a (t u i) -> p a u t i", t=4, i=8),
-            w3_raw[:].rearrange("p a (u i t) -> p a u t i", t=4, i=8),
-        )
-        do_behind(1, 0)
-        gain_h(0, 0, J)
-        do_behind(1, 1)
+                ahead_half(b, t, h)
+        cast_w1(1, 0)
+        quant_w1(1, 0)
+        cast_w1(0, 1, "win3")
+        for h in range(2):
+            ahead_half(1, 1, h)
+        quant_w1(0, 1)
+        for h in range(2):
+            ahead_half(1, 2, h)
+        cast_w1(1, 1, "win5")
+        for h in range(2):
+            ahead_half(1, 3, h)
+        quant_w1(1, 1)
+
+        behind = {0: behind_all(0, 0), 1: behind_all(0, 1)}
+        for t in range(4):
+            behind[t + 2] = behind_all((t + 2) // 4, (t + 2) % 4)
+            contrast(behind[t], 0, t, 0, J)
+        behind[6] = behind_all(1, 2)
+        log_h(0, 0, 256)
+        contrast(behind[4], 1, 0, 0, 256)
+        behind[7] = behind_all(1, 3)
+        log_h(0, 256, J)
+        contrast(behind[5], 1, 1, 0, 256)
+        gain_h(0, 0, 256)
+        contrast(behind[6], 1, 2, 0, 256)
+        gain_h(0, 256, J)
+        contrast(behind[7], 1, 3, 0, 256)
         quant_h(0, 0, J)
-        do_behind(1, 2)
-        last = behind_all(1, 3)
 
         y = held([P, 4, J], F32, "y")
         y_g = held([P, 4 * J], BF16, "y_g")
@@ -275,19 +288,40 @@ def tile_list_ring_contrast_forecast_kernel(
                 out=y_c[:, cols].bitcast(FP8X4), scales=y_s[:, cols], in_=y_g[:, 512 * c : 512 * (c + 1)]
             )
 
-        for step in range(9):
-            if step < 4:
-                contrast(last, 1, 3, 128 * step, 128 * (step + 1))
-            if 0 <= step - 3 < 4:
-                quant_h(1, 128 * (step - 3), 128 * (step - 2))
-                third(step - 3)
-            if 0 <= step - 2 < 4:
-                gain_h(1, 128 * (step - 2), 128 * (step - 1))
-            if 0 <= step - 5 < 4:
-                quant_y(step - 5)
-            if 0 <= step - 4 < 4:
-                round_y(step - 4)
-        nc.sync.dma_start(out_words, y_c[:].bitcast(I32))
+        def store_words(c0, c1):
+            nc.sync.dma_start(out_words[:, c0:c1], y_c[:, c0:c1].bitcast(I32))
+
+        log_h(1, 0, 128)
+        log_h(1, 128, 256)
+        contrast(behind[4], 1, 0, 256, J)
+        gain_h(1, 0, 128)
+        contrast(behind[5], 1, 1, 256, J)
+        quant_h(1, 0, 128)
+        third(0)
+        gain_h(1, 128, 256)
+        contrast(behind[6], 1, 2, 256, J)
+        quant_h(1, 128, 256)
+        third(1)
+        contrast(behind[7], 1, 3, 256, 384)
+        log_h(1, 256, 384)
+        contrast(behind[7], 1, 3, 384, J)
+        log_h(1, 384, J)
+        round_y(0)
+        gain_h(1, 256, 384)
+        quant_y(0)
+        quant_h(1, 256, 384)
+        third(2)
+        gain_h(1, 384, J)
+        round_y(1)
+        quant_h(1, 384, J)
+        third(3)
+        quant_y(1)
+        store_words(0, 256)
+        round_y(2)
+        quant_y(2)
+        round_y(3)
+        quant_y(3)
+        store_words(256, J)
         for q in range(4):
             eng = nc.scalar if q % 2 else nc.sync
             eng.dma_start(out_2[0, 4 * q : 4 * q + 4, :].bitcast(I32), y_s[32 * q : 32 * q + 4, :].bitcast(I32))

@@ -17,7 +17,8 @@ FP4X4 = mybir.dt.float4_e2m1fn_x4
 ACT = mybir.ActivationFunctionType
 ALU = mybir.AluOpType
 
-CASTS = {(0, 0): "s", (1, 0): "s", (0, 1): "v", (1, 1): "v"}
+OPEN = ((0, 0), (0, 1))
+CASTS = {(0, 0): "g", (1, 0): "g", (0, 1): "g", (1, 1): "s"}
 
 
 def tile_list_ring_contrast_forecast_kernel(
@@ -38,8 +39,8 @@ def tile_list_ring_contrast_forecast_kernel(
         pos2_t = lists.tile([P, J // 16], U16, name="pos2_t")
 
         tab_s = held([P, T], U8, "tab_s")
-        w_s_raw = held([P, H], U8, "w_s_raw")
-        planes = held([P, 2, S + H], U8, "planes")
+        w_s_raw = held([P, H + N], U8, "w_s_raw")
+        planes = held([P, 2, S + H + N], U8, "planes")
         nc.vector.memset(w_s_raw[0:96, :].bitcast(I32), 0)
         nc.vector.memset(tab_s[0:96, :].bitcast(I32), 0)
         nc.gpsimd.memset(planes[:].bitcast(I32), 0)
@@ -49,53 +50,48 @@ def tile_list_ring_contrast_forecast_kernel(
         nc.scalar.activation(warm[:], warm_in[:], ACT.Ln)
 
         nc.sync.dma_start(offs_t[:], offs)
-        nc.sync.dma_start(w_s_raw[96:128, :].bitcast(I32), w2_scales.bitcast(I32).rearrange("a q c -> q a c"))
+        nc.sync.dma_start(w_s_raw[96:128, 0:H].bitcast(I32), w2_scales.bitcast(I32).rearrange("a q c -> q a c"))
+        nc.sync.dma_start(w_s_raw[96:128, H : H + N].bitcast(I32), w3_scales.bitcast(I32).rearrange("a q c -> q a c"))
         nc.sync.dma_start(tab_s[96:128, :].bitcast(I32), tab_scales.bitcast(I32).rearrange("a q c -> q a c"))
         tab_w = [held([P, T], U16, f"tab_w{a}") for a in range(2)]
         nc.sync.dma_start(tab_w[0][:].bitcast(I32), tab_words[0].bitcast(I32))
-        w2_raw = [held([P, 2, 512], I32, "w2_raw0")]
+        w2_raw = [held([P, 2, 512], I32, f"w2_raw{b}") for b in range(2)]
         w2_src = w2_words.rearrange("a p c i -> p a (c i)").bitcast(I32)
-        nc.sync.dma_start(w2_raw[0][:], w2_src[:, :, 0:512])
+        for b in range(2):
+            nc.sync.dma_start(w2_raw[b][:], w2_src[:, :, 512 * b : 512 * (b + 1)])
         nc.sync.dma_start(pos2_t[:], pos2)
         nc.sync.dma_start(pos1_t[:], pos1)
         nc.sync.dma_start(tab_w[1][:].bitcast(I32), tab_words[1].bitcast(I32))
+        w3_raw = held([P, 2, N], U16, "w3_raw")
+        nc.sync.dma_start(w3_raw[:].bitcast(I32), w3_words.bitcast(I32).rearrange("a p c -> p a c"))
 
         def deal_bytes(dst, src):
             nc.vector.tensor_copy(
-                dst.rearrange("p (b t u i) -> p b u t i", t=4, u=8, i=16),
-                src.rearrange("p (b u i t) -> p b u t i", t=4, u=8, i=16),
+                dst.rearrange("p (b t u i) -> p u b t i", t=4, u=8, i=16),
+                src.rearrange("p (b u i t) -> p u b t i", t=4, u=8, i=16),
             )
 
-        rows = held([P, S + H], U8, "rows")
-        deal_bytes(rows[:, S : S + H], w_s_raw[:])
+        rows = held([P, S + H + N], U8, "rows")
+        deal_bytes(rows[:, S:], w_s_raw[:])
         gain_t = held([P, 2, 4], F32, "gain_t", "w_s_raw")
         nc.sync.dma_start(gain_t[:], gain.rearrange("(b p t) -> p b t", b=2, t=4))
         v_s_rows = held([P, S], U8, "v_s_rows")
         nc.vector.tensor_copy(v_s_rows[:], tab_s[:].indirect(offs_t[:]))
-        w3_raw = held([P, 2, N], U16, "w3_raw", "tab_s")
-        nc.sync.dma_start(w3_raw[:].bitcast(I32), w3_words.bitcast(I32).rearrange("a p c -> p a c"))
         nc.vector.tensor_copy(rows[:, 0:S].bitcast(I32), v_s_rows[:].bitcast(I32))
         for q in range(4):
             nc.scalar.dma_start(
                 planes[32 * q : 32 * q + 4].bitcast(I32), rows[96 + 8 * q : 104 + 8 * q, :].bitcast(I32)
             )
-        w3_s_raw = held([P, 2 * N], U8, "w3_s_raw", "v_s_rows")
-        nc.gpsimd.memset(w3_s_raw[:].bitcast(I32), 0)
-        for q in range(4):
-            nc.sync.dma_start(
-                w3_s_raw[32 * q : 32 * q + 4, :].bitcast(I32).rearrange("r (a c) -> r a c", a=2),
-                w3_scales[:, 4 * q : 4 * q + 4, :].bitcast(I32).rearrange("a r c -> r a c"),
-            )
-        w2_raw.append(held([P, 2, 512], I32, "w2_raw1", "rows"))
-        nc.sync.dma_start(w2_raw[1][:], w2_src[:, :, 512:1024])
+        w1_all = held([P, 4 * 2048], F32, "w1_all", "rows")
         w1_raw = {}
-
-        def load_w1(a, b, tag):
-            w1_raw[a, b] = held([P, 4, 512], F32, f"w1_raw{a}{b}", tag)
-            nc.sync.dma_start(
-                w1_raw[a, b][:],
-                w1[512 * a : 512 * (a + 1), 512 * b : 512 * (b + 1)].rearrange("(p j) c -> p j c", j=4),
-            )
+        for b in range(2):
+            for a in range(2):
+                c0 = 2048 * (2 * b + a)
+                w1_raw[a, b] = w1_all[:, c0 : c0 + 2048].rearrange("p (j c) -> p j c", j=4)
+                nc.sync.dma_start(
+                    w1_raw[a, b],
+                    w1[512 * a : 512 * (a + 1), 512 * b : 512 * (b + 1)].rearrange("(p j) c -> p j c", j=4),
+                )
 
         v_w = [[held([P, 512], U16, f"v_w{a}{h}") for h in range(2)] for a in range(2)]
 
@@ -113,15 +109,11 @@ def tile_list_ring_contrast_forecast_kernel(
 
         gather_words(0, 0)
         deal_w2(0, "w2_c0")
-        load_w1(0, 0, "w2_raw0")
-        gather_words(1, 0)
         gather_words(0, 1)
-        load_w1(1, 0, "tab_w0")
+        deal_w2(1, "tab_w0")
+        gather_words(1, 0)
         gather_words(1, 1)
-        load_w1(0, 1, "tab_w1")
-        w3_s = held([P, 2, N], U8, "w3_s")
-        w3_c = held([P, 2, N], U16, "w3_c")
-        deal_bytes(w3_s[:].rearrange("p a c -> p (a c)"), w3_s_raw[:])
+        w3_c = held([P, 2, N], U16, "w3_c", "tab_w1")
         nc.vector.tensor_copy(
             w3_c[:].rearrange("p a (t u i) -> p a u t i", t=4, i=8),
             w3_raw[:].rearrange("p a (u i t) -> p a u t i", t=4, i=8),
@@ -131,11 +123,14 @@ def tile_list_ring_contrast_forecast_kernel(
         w1_s = {}
         w1_g = {}
 
-        def cast_w1(a, b, tag=None):
-            g = held([P, 4 * 512], BF16, f"w1_g{a}{b}", tag)
-            w1_g[a, b] = g
-            dst = g[:].rearrange("p (t m j) -> p m t j", t=4, j=4)
-            src = w1_raw[a, b][:].rearrange("p j (m t) -> p m t j", t=4)
+        early = held([P, 5 * J], F32, "early")
+        for a in range(2):
+            w1_g[a, 0] = held([P, 4 * 512], BF16, f"w1_g{a}")[:]
+            w1_g[a, 1] = early[:, J + 1024 * a : J + 1024 * (a + 1)].bitcast(BF16)
+
+        def cast_w1(a, b):
+            dst = w1_g[a, b].rearrange("p (t m j) -> p m t j", t=4, j=4)
+            src = w1_raw[a, b].rearrange("p j (m t) -> p m t j", t=4)
             if CASTS[a, b] == "v":
                 nc.vector.tensor_copy(dst, src)
             elif CASTS[a, b] == "g":
@@ -146,55 +141,57 @@ def tile_list_ring_contrast_forecast_kernel(
                 for u in range(2):
                     nc.scalar.copy(dst[:, 64 * u : 64 * (u + 1)], src[:, 64 * u : 64 * (u + 1)])
 
-        def quant_w1(a, b):
-            w1_c[a, b] = held([P, 512], U32, f"w1_c{a}{b}")
+        def quant_w1(a, b, tag):
+            w1_c[a, b] = held([P, 512], U32, f"w1_c{a}{b}", tag)
             w1_s[a, b] = held([P, 512], U8, f"w1_s{a}{b}")
-            nc.vector.quantize_mx(out=w1_c[a, b][:].bitcast(FP8X4), scales=w1_s[a, b][:], in_=w1_g[a, b][:])
+            nc.vector.quantize_mx(out=w1_c[a, b][:].bitcast(FP8X4), scales=w1_s[a, b][:], in_=w1_g[a, b])
 
-        def first_half(window, h, codes, scales):
-            acc = psum.tile([P, 512], F32, name="acc")
-            for a in range(2):
-                nc.tensor.matmul_mx(
-                    out=acc[:], lhsT=codes(a).bitcast(FP8X4), lhsT_scale=scales(a),
-                    rhs=v_w[a][h][:].bitcast(FP4X4), rhs_scale=planes[:, a, 512 * h : 512 * (h + 1)],
-                    start=(a == 0), stop=(a == 1),
-                )
+        def first_pass(acc, a, h, codes, scales):
+            nc.tensor.matmul_mx(
+                out=acc[:], lhsT=codes.bitcast(FP8X4), lhsT_scale=scales,
+                rhs=v_w[a][h][:].bitcast(FP4X4), rhs_scale=planes[:, a, 512 * h : 512 * (h + 1)],
+                start=(a == 0), stop=(a == 1),
+            )
+
+        def first_half(window, h, codes, scales, acc=None):
+            if acc is None:
+                acc = psum.tile([P, 512], F32, name="acc")
+                first_pass(acc, 0, h, codes(0), scales(0))
+            first_pass(acc, 1, h, codes(1), scales(1))
             nc.scalar.copy(window[:, 512 * h : 512 * (h + 1)], acc[:])
 
         ahead = {}
         ahead_all = {}
 
-        def ahead_half(b, t, h):
+        def ahead_half(b, t, h, acc=None):
             if h == 0:
                 ahead_all[b, t] = held([P, S], F32, f"ahead_all{b}{t}", f"win{4 * b + t}")
             cols = slice(128 * t, 128 * (t + 1))
-            first_half(ahead_all[b, t], h, lambda a: w2_c[b][:, a, cols], lambda a: planes[:, a, S + 512 * b + 128 * t : S + 512 * b + 128 * (t + 1)])
+            first_half(ahead_all[b, t], h, lambda a: w2_c[b][:, a, cols], lambda a: planes[:, a, S + 512 * b + 128 * t : S + 512 * b + 128 * (t + 1)], acc)
             if h == 1:
-                ahead[b, t] = held([P, J], F32, f"ahead{b}{t}")
+                ahead[b, t] = held([P, J], F32, f"ahead{b}{t}", "w1_g1" if (b, t) == (1, 3) else None)
                 nc.vector.tensor_copy(ahead[b, t][:], ahead_all[b, t][:].indirect(pos2_t[:]))
 
-        squares_all = [held([P, 4, J], F32, f"squares{b}") for b in range(2)]
-        squares = [[squares_all[b][:, t, :] for t in range(4)] for b in range(2)]
+        squares = [early[:, 0 : 4 * J].rearrange("p (t j) -> p t j", t=4), held([P, 4, J], F32, "squares1")[:]]
+        logs = held([P, J, 4], F32, "logs")
 
         def behind_all(b, t):
-            window = held([P, S], F32, f"behind_all{b}{t}", f"win{(1, 2, 0, 4, 6, 7, 1, 2)[4 * b + t]}")
+            window = held([P, S], F32, f"behind_all{b}{t}", f"win{(0, 1, 3, 4, 8, 0, 1, 3)[4 * b + t]}")
             cols = slice(128 * t, 128 * (t + 1))
             for h in range(2):
                 first_half(window, h, lambda a: w1_c[a, b][:, cols], lambda a: w1_s[a, b][:, cols])
             return window
 
         def contrast(window, b, t, c0, c1):
-            diff = squares[b][t][:, c0:c1]
+            diff = squares[b][:, t, c0:c1]
             nc.vector.tensor_tensor(
                 diff, window[:].indirect(pos1_t[:, c0 // 16 : c1 // 16]), ahead[b, t][:, c0:c1], ALU.subtract
             )
             nc.scalar.activation(diff, diff, ACT.Square)
 
-        logs = held([P, J, 4], F32, "logs")
-
         def log_h(b, c0, c1):
             nc.scalar.activation(
-                logs[:, c0:c1, :], squares_all[b][:, :, c0:c1].rearrange("p t j -> p j t"), ACT.Ln, bias=1.0
+                logs[:, c0:c1, :], squares[b][:, :, c0:c1].rearrange("p t j -> p j t"), ACT.Ln, bias=1.0
             )
 
         h_c = [held([P, J], U32, f"h_c{b}") for b in range(2)]
@@ -214,44 +211,42 @@ def tile_list_ring_contrast_forecast_kernel(
                 out=h_c[b][:, c0:c1].bitcast(FP8X4), scales=h_s[b][:, c0:c1], in_=h_g[b][:, 4 * c0 : 4 * c1]
             )
 
-        for t, h in ((0, 0), (1, 0), (0, 1)):
-            ahead_half(0, t, h)
-        deal_w2(1, "win0")
-        load_w1(1, 1, "rows")
-        for t, h in ((1, 1), (2, 0), (2, 1)):
-            ahead_half(0, t, h)
-        cast_w1(0, 0)
-        quant_w1(0, 0)
-        for b, t in ((0, 3), (1, 0)):
+        opened = {}
+        for t, h in OPEN:
+            opened[t, h] = psum.tile([P, 512], F32, name="acc")
+            first_pass(opened[t, h], 0, h, w2_c[0][:, 0, 128 * t : 128 * (t + 1)], planes[:, 0, S + 128 * t : S + 128 * (t + 1)])
+        for t in range(4):
             for h in range(2):
-                ahead_half(b, t, h)
-        cast_w1(1, 0)
-        quant_w1(1, 0)
-        cast_w1(0, 1, "win3")
+                ahead_half(0, t, h, opened.get((t, h)))
+        for a, b in ((0, 0), (1, 0), (0, 1)):
+            cast_w1(a, b)
+        quant_w1(0, 0, "win2")
+        for h in range(2):
+            ahead_half(1, 0, h)
         for h in range(2):
             ahead_half(1, 1, h)
-        quant_w1(0, 1)
-        for h in range(2):
-            ahead_half(1, 2, h)
-        cast_w1(1, 1, "win5")
-        for h in range(2):
-            ahead_half(1, 3, h)
-        quant_w1(1, 1)
+        quant_w1(1, 0, "win5")
+        for t in range(2, 4):
+            for h in range(2):
+                ahead_half(1, t, h)
+        cast_w1(1, 1)
+        quant_w1(1, 1, "win6")
 
         behind = {0: behind_all(0, 0), 1: behind_all(0, 1)}
         for t in range(4):
             behind[t + 2] = behind_all((t + 2) // 4, (t + 2) % 4)
             contrast(behind[t], 0, t, 0, J)
-        behind[6] = behind_all(1, 2)
+            if t == 0:
+                quant_w1(0, 1, "win7")
         log_h(0, 0, 256)
-        contrast(behind[4], 1, 0, 0, 256)
-        behind[7] = behind_all(1, 3)
+        behind[6] = behind_all(1, 2)
+        contrast(behind[4], 1, 0, 0, J)
         log_h(0, 256, J)
-        contrast(behind[5], 1, 1, 0, 256)
         gain_h(0, 0, 256)
-        contrast(behind[6], 1, 2, 0, 256)
+        behind[7] = behind_all(1, 3)
+        contrast(behind[5], 1, 1, 0, J)
         gain_h(0, 256, J)
-        contrast(behind[7], 1, 3, 0, 256)
+        contrast(behind[6], 1, 2, 0, J)
         quant_h(0, 0, J)
 
         y = held([P, 4, J], F32, "y")
@@ -261,6 +256,8 @@ def tile_list_ring_contrast_forecast_kernel(
         out_rows = out_0.rearrange("(p t) j -> p t j", t=4)
         out_words = out_1[0].rearrange("p m i -> p (m i)").bitcast(I32)
 
+        sums = {}
+
         def third(c):
             cols = slice(128 * c, 128 * (c + 1))
             acc = psum.tile([P, 512], F32, name="acc")
@@ -269,12 +266,22 @@ def tile_list_ring_contrast_forecast_kernel(
                     nc.tensor.matmul_mx(
                         out=acc[:, 128 * t : 128 * (t + 1)],
                         lhsT=w3_c[:, b, 128 * t : 128 * (t + 1)].bitcast(FP4X4),
-                        lhsT_scale=w3_s[:, b, 128 * t : 128 * (t + 1)],
+                        lhsT_scale=planes[:, b, S + H + 128 * t : S + H + 128 * (t + 1)],
                         rhs=h_c[b][:, cols].bitcast(FP8X4), rhs_scale=h_s[b][:, cols],
                         start=(b == 0), stop=(b == 1),
                     )
-            nc.scalar.copy(y[:, :, cols], acc[:].rearrange("p (t j) -> p t j", t=4))
+            sums[c] = acc
+
+        def store_y(c):
+            cols = slice(128 * c, 128 * (c + 1))
+            nc.scalar.copy(y[:, :, cols], sums[c][:].rearrange("p (t j) -> p t j", t=4))
             nc.sync.dma_start(out_rows[:, :, cols], y[:, :, cols])
+
+        def round_sums(c):
+            nc.scalar.copy(
+                y_g[:, 512 * c : 512 * (c + 1)].rearrange("p (j t) -> p j t", t=4),
+                sums[c][:].rearrange("p (t j) -> p j t", t=4),
+            )
 
         def round_y(c):
             nc.vector.tensor_copy(
@@ -282,46 +289,30 @@ def tile_list_ring_contrast_forecast_kernel(
                 y[:, :, 128 * c : 128 * (c + 1)].rearrange("p t (u i) -> p u t i", i=4),
             )
 
-        def quant_y(c):
-            cols = slice(128 * c, 128 * (c + 1))
+        def quant_y(c, n=1):
+            cols = slice(128 * c, 128 * (c + n))
             nc.vector.quantize_mx(
-                out=y_c[:, cols].bitcast(FP8X4), scales=y_s[:, cols], in_=y_g[:, 512 * c : 512 * (c + 1)]
+                out=y_c[:, cols].bitcast(FP8X4), scales=y_s[:, cols], in_=y_g[:, 512 * c : 512 * (c + n)]
             )
 
         def store_words(c0, c1):
             nc.sync.dma_start(out_words[:, c0:c1], y_c[:, c0:c1].bitcast(I32))
 
-        log_h(1, 0, 128)
-        log_h(1, 128, 256)
-        contrast(behind[4], 1, 0, 256, J)
-        gain_h(1, 0, 128)
-        contrast(behind[5], 1, 1, 256, J)
-        quant_h(1, 0, 128)
-        third(0)
-        gain_h(1, 128, 256)
-        contrast(behind[6], 1, 2, 256, J)
-        quant_h(1, 128, 256)
-        third(1)
-        contrast(behind[7], 1, 3, 256, 384)
-        log_h(1, 256, 384)
-        contrast(behind[7], 1, 3, 384, J)
-        log_h(1, 384, J)
-        round_y(0)
-        gain_h(1, 256, 384)
-        quant_y(0)
-        quant_h(1, 256, 384)
-        third(2)
-        gain_h(1, 384, J)
-        round_y(1)
-        quant_h(1, 384, J)
-        third(3)
-        quant_y(1)
-        store_words(0, 256)
-        round_y(2)
-        quant_y(2)
-        round_y(3)
-        quant_y(3)
-        store_words(256, J)
+        for c in range(4):
+            contrast(behind[7], 1, 3, 128 * c, 128 * (c + 1))
+            log_h(1, 128 * c, 128 * (c + 1))
+        for c in range(5):
+            if c < 4:
+                gain_h(1, 128 * c, 128 * (c + 1))
+            if c > 0:
+                quant_h(1, 128 * (c - 1), 128 * c)
+                third(c - 1)
+        for c in range(4):
+            store_y(c)
+            round_y(c)
+            if c % 2:
+                quant_y(c - 1, 2)
+                store_words(128 * (c - 1), 128 * (c + 1))
         for q in range(4):
             eng = nc.scalar if q % 2 else nc.sync
             eng.dma_start(out_2[0, 4 * q : 4 * q + 4, :].bitcast(I32), y_s[32 * q : 32 * q + 4, :].bitcast(I32))

@@ -4,6 +4,9 @@ import concourse.mybir as mybir
 
 K, H, N, T, S, J = 1024, 1024, 512, 4096, 1024, 512
 P = 128
+PASS = 512
+CHUNK = 128
+TOP = 96
 FLOPS = 2 * (2 * K * H * S + H * N * J)
 
 F32 = mybir.dt.float32
@@ -17,8 +20,7 @@ FP4X4 = mybir.dt.float4_e2m1fn_x4
 ACT = mybir.ActivationFunctionType
 ALU = mybir.AluOpType
 
-OPEN = ((0, 0), (0, 1))
-CASTS = {(0, 0): "g", (1, 0): "g", (0, 1): "g", (1, 1): "s"}
+BEHIND_SLOTS = (0, 1, 3, 4, 8)
 
 
 def tile_list_ring_contrast_forecast_kernel(
@@ -41,70 +43,69 @@ def tile_list_ring_contrast_forecast_kernel(
         tab_s = held([P, T], U8, "tab_s")
         w_s_raw = held([P, H + N], U8, "w_s_raw")
         planes = held([P, 2, S + H + N], U8, "planes")
-        nc.vector.memset(w_s_raw[0:96, :].bitcast(I32), 0)
-        nc.vector.memset(tab_s[0:96, :].bitcast(I32), 0)
+        nc.vector.memset(w_s_raw[0:TOP, :].bitcast(I32), 0)
+        nc.vector.memset(tab_s[0:TOP, :].bitcast(I32), 0)
         nc.gpsimd.memset(planes[:].bitcast(I32), 0)
-        warm_in = held([P, 2], F32, "warm_in")
-        nc.gpsimd.memset(warm_in[:], 1.0)
-        warm = held([P, 2], F32, "warm")
-        nc.scalar.activation(warm[:], warm_in[:], ACT.Ln)
+        one = held([P, 1], F32, "one")
+        nc.gpsimd.memset(one[:], 1.0)
+        zero = held([P, 1], F32, "zero")
+        nc.scalar.activation(zero[:], one[:], ACT.Ln)
 
         nc.sync.dma_start(offs_t[:], offs)
-        nc.sync.dma_start(w_s_raw[96:128, 0:H].bitcast(I32), w2_scales.bitcast(I32).rearrange("a q c -> q a c"))
-        nc.sync.dma_start(w_s_raw[96:128, H : H + N].bitcast(I32), w3_scales.bitcast(I32).rearrange("a q c -> q a c"))
-        nc.sync.dma_start(tab_s[96:128, :].bitcast(I32), tab_scales.bitcast(I32).rearrange("a q c -> q a c"))
+        nc.sync.dma_start(w_s_raw[TOP:P, 0:H].bitcast(I32), w2_scales.bitcast(I32).rearrange("a q r -> q a r"))
+        nc.sync.dma_start(w_s_raw[TOP:P, H : H + N].bitcast(I32), w3_scales.bitcast(I32).rearrange("b q n -> q b n"))
+        nc.sync.dma_start(tab_s[TOP:P, :].bitcast(I32), tab_scales.bitcast(I32).rearrange("a q s -> q a s"))
         tab_w = [held([P, T], U16, f"tab_w{a}") for a in range(2)]
         nc.sync.dma_start(tab_w[0][:].bitcast(I32), tab_words[0].bitcast(I32))
-        w2_raw = [held([P, 2, 512], I32, f"w2_raw{b}") for b in range(2)]
-        w2_src = w2_words.rearrange("a p c i -> p a (c i)").bitcast(I32)
+        w2_raw = [held([P, 2, PASS], I32, f"w2_raw{b}") for b in range(2)]
+        w2_src = w2_words.rearrange("a p r i -> p a (r i)").bitcast(I32)
         for b in range(2):
-            nc.sync.dma_start(w2_raw[b][:], w2_src[:, :, 512 * b : 512 * (b + 1)])
+            nc.sync.dma_start(w2_raw[b][:], w2_src[:, :, PASS * b : PASS * (b + 1)])
         nc.sync.dma_start(pos2_t[:], pos2)
         nc.sync.dma_start(pos1_t[:], pos1)
         nc.sync.dma_start(tab_w[1][:].bitcast(I32), tab_words[1].bitcast(I32))
         w3_raw = held([P, 2, N], U16, "w3_raw")
-        nc.sync.dma_start(w3_raw[:].bitcast(I32), w3_words.bitcast(I32).rearrange("a p c -> p a c"))
-
-        def deal_bytes(dst, src):
-            nc.vector.tensor_copy(
-                dst.rearrange("p (b t u i) -> p u b t i", t=4, u=8, i=16),
-                src.rearrange("p (b u i t) -> p u b t i", t=4, u=8, i=16),
-            )
+        nc.sync.dma_start(w3_raw[:].bitcast(I32), w3_words.bitcast(I32).rearrange("b p n -> p b n"))
 
         rows = held([P, S + H + N], U8, "rows")
-        deal_bytes(rows[:, S:], w_s_raw[:])
+        nc.vector.tensor_copy(
+            rows[:, S:].rearrange("p (x t u e) -> p u x t e", t=4, u=8, e=16),
+            w_s_raw[:].rearrange("p (x u e t) -> p u x t e", t=4, u=8, e=16),
+        )
         gain_t = held([P, 2, 4], F32, "gain_t", "w_s_raw")
         nc.sync.dma_start(gain_t[:], gain.rearrange("(b p t) -> p b t", b=2, t=4))
-        v_s_rows = held([P, S], U8, "v_s_rows")
-        nc.vector.tensor_copy(v_s_rows[:], tab_s[:].indirect(offs_t[:]))
-        nc.vector.tensor_copy(rows[:, 0:S].bitcast(I32), v_s_rows[:].bitcast(I32))
-        for q in range(4):
+        picked_s = held([P, S], U8, "picked_s")
+        nc.vector.tensor_copy(picked_s[:], tab_s[:].indirect(offs_t[:]))
+        nc.vector.tensor_copy(rows[:, 0:S].bitcast(I32), picked_s[:].bitcast(I32))
+        for quad in range(4):
             nc.scalar.dma_start(
-                planes[32 * q : 32 * q + 4].bitcast(I32), rows[96 + 8 * q : 104 + 8 * q, :].bitcast(I32)
+                planes[32 * quad : 32 * quad + 4].bitcast(I32),
+                rows[TOP + 8 * quad : TOP + 8 * quad + 8, :].bitcast(I32),
             )
-        w1_all = held([P, 4 * 2048], F32, "w1_all", "rows")
+        w1_all = held([P, 4 * 4 * PASS], F32, "w1_all", "rows")
         w1_raw = {}
         for b in range(2):
             for a in range(2):
-                c0 = 2048 * (2 * b + a)
-                w1_raw[a, b] = w1_all[:, c0 : c0 + 2048].rearrange("p (j c) -> p j c", j=4)
+                first = 4 * PASS * (2 * b + a)
+                w1_raw[a, b] = w1_all[:, first : first + 4 * PASS].rearrange("p (i r) -> p i r", i=4)
                 nc.sync.dma_start(
                     w1_raw[a, b],
-                    w1[512 * a : 512 * (a + 1), 512 * b : 512 * (b + 1)].rearrange("(p j) c -> p j c", j=4),
+                    w1[PASS * a : PASS * (a + 1), PASS * b : PASS * (b + 1)].rearrange("(p i) r -> p i r", i=4),
                 )
 
-        v_w = [[held([P, 512], U16, f"v_w{a}{h}") for h in range(2)] for a in range(2)]
+        picked_w = [[held([P, PASS], U16, f"picked_w{a}{half}") for half in range(2)] for a in range(2)]
 
-        def gather_words(a, h):
-            nc.vector.tensor_copy(v_w[a][h][:], tab_w[a][:].indirect(offs_t[:, 32 * h : 32 * (h + 1)]))
+        def gather_words(a, half):
+            entries = offs_t[:, PASS // 16 * half : PASS // 16 * (half + 1)]
+            nc.vector.tensor_copy(picked_w[a][half][:], tab_w[a][:].indirect(entries))
 
         w2_c = {}
 
         def deal_w2(b, tag):
-            w2_c[b] = held([P, 2, 512], I32, f"w2_c{b}", tag)
+            w2_c[b] = held([P, 2, PASS], I32, f"w2_c{b}", tag)
             nc.vector.tensor_copy(
-                w2_c[b][:].rearrange("p a (t u i) -> p a u t i", t=4, i=4),
-                w2_raw[b][:].rearrange("p a (u i t) -> p a u t i", t=4, i=4),
+                w2_c[b][:].rearrange("p a (t u e) -> p a u t e", t=4, e=4),
+                w2_raw[b][:].rearrange("p a (u e t) -> p a u t e", t=4, e=4),
             )
 
         gather_words(0, 0)
@@ -115,204 +116,195 @@ def tile_list_ring_contrast_forecast_kernel(
         gather_words(1, 1)
         w3_c = held([P, 2, N], U16, "w3_c", "tab_w1")
         nc.vector.tensor_copy(
-            w3_c[:].rearrange("p a (t u i) -> p a u t i", t=4, i=8),
-            w3_raw[:].rearrange("p a (u i t) -> p a u t i", t=4, i=8),
+            w3_c[:].rearrange("p b (t u e) -> p b u t e", t=4, e=8),
+            w3_raw[:].rearrange("p b (u e t) -> p b u t e", t=4, e=8),
         )
 
         w1_c = {}
         w1_s = {}
-        w1_g = {}
+        w1_g = {(a, 0): held([P, 4 * PASS], BF16, f"w1_g{a}")[:] for a in range(2)}
 
-        early = held([P, 5 * J], F32, "early")
-        for a in range(2):
-            w1_g[a, 0] = held([P, 4 * 512], BF16, f"w1_g{a}")[:]
-            w1_g[a, 1] = early[:, J + 1024 * a : J + 1024 * (a + 1)].bitcast(BF16)
+        def w1_views(a, b):
+            return (
+                w1_g[a, b].rearrange("p (t m i) -> p m t i", t=4, i=4),
+                w1_raw[a, b].rearrange("p i (m t) -> p m t i", t=4),
+            )
 
-        def cast_w1(a, b):
-            dst = w1_g[a, b].rearrange("p (t m j) -> p m t j", t=4, j=4)
-            src = w1_raw[a, b].rearrange("p j (m t) -> p m t j", t=4)
-            if CASTS[a, b] == "v":
-                nc.vector.tensor_copy(dst, src)
-            elif CASTS[a, b] == "g":
-                for u in range(4):
-                    part = slice(32 * u, 32 * (u + 1))
-                    nc.gpsimd.tensor_scalar(dst[:, part], src[:, part], 1.0, 0.0, ALU.mult, ALU.add)
-            else:
-                for u in range(2):
-                    nc.scalar.copy(dst[:, 64 * u : 64 * (u + 1)], src[:, 64 * u : 64 * (u + 1)])
+        def round_w1_on_gpsimd(a, b):
+            dst, src = w1_views(a, b)
+            for piece in range(4):
+                part = slice(32 * piece, 32 * (piece + 1))
+                nc.gpsimd.tensor_scalar(dst[:, part], src[:, part], 1.0, 0.0, ALU.mult, ALU.add)
 
-        def quant_w1(a, b, tag):
-            w1_c[a, b] = held([P, 512], U32, f"w1_c{a}{b}", tag)
-            w1_s[a, b] = held([P, 512], U8, f"w1_s{a}{b}")
+        def round_w1_on_vector(a, b):
+            dst, src = w1_views(a, b)
+            nc.vector.tensor_copy(dst, src)
+
+        def quantise_w1(a, b, tag=None):
+            w1_c[a, b] = held([P, PASS], U32, f"w1_c{a}{b}", tag)
+            w1_s[a, b] = held([P, PASS], U8, f"w1_s{a}{b}")
             nc.vector.quantize_mx(out=w1_c[a, b][:].bitcast(FP8X4), scales=w1_s[a, b][:], in_=w1_g[a, b])
 
-        def first_pass(acc, a, h, codes, scales):
+        def w1_slice(a, b, t):
+            return w1_c[a, b][:, P * t : P * (t + 1)], w1_s[a, b][:, P * t : P * (t + 1)]
+
+        def w2_slice(a, b, t):
+            first = S + PASS * b + P * t
+            return w2_c[b][:, a, P * t : P * (t + 1)], planes[:, a, first : first + P]
+
+        def reading_pass(acc, weight_slice, a, b, t, half):
+            codes, scales = weight_slice(a, b, t)
             nc.tensor.matmul_mx(
                 out=acc[:], lhsT=codes.bitcast(FP8X4), lhsT_scale=scales,
-                rhs=v_w[a][h][:].bitcast(FP4X4), rhs_scale=planes[:, a, 512 * h : 512 * (h + 1)],
+                rhs=picked_w[a][half][:].bitcast(FP4X4), rhs_scale=planes[:, a, PASS * half : PASS * (half + 1)],
                 start=(a == 0), stop=(a == 1),
             )
 
-        def first_half(window, h, codes, scales, acc=None):
-            if acc is None:
-                acc = psum.tile([P, 512], F32, name="acc")
-                first_pass(acc, 0, h, codes(0), scales(0))
-            first_pass(acc, 1, h, codes(1), scales(1))
-            nc.scalar.copy(window[:, 512 * h : 512 * (h + 1)], acc[:])
+        def open_reading(weight_slice, b, t, half):
+            acc = psum.tile([P, PASS], F32, name="acc")
+            reading_pass(acc, weight_slice, 0, b, t, half)
+            return acc
+
+        def close_reading(acc, weight_slice, b, t, half, full):
+            reading_pass(acc, weight_slice, 1, b, t, half)
+            nc.scalar.copy(full[:, PASS * half : PASS * (half + 1)], acc[:])
 
         ahead = {}
-        ahead_all = {}
 
-        def ahead_half(b, t, h, acc=None):
-            if h == 0:
-                ahead_all[b, t] = held([P, S], F32, f"ahead_all{b}{t}", f"win{4 * b + t}")
-            cols = slice(128 * t, 128 * (t + 1))
-            first_half(ahead_all[b, t], h, lambda a: w2_c[b][:, a, cols], lambda a: planes[:, a, S + 512 * b + 128 * t : S + 512 * b + 128 * (t + 1)], acc)
-            if h == 1:
-                ahead[b, t] = held([P, J], F32, f"ahead{b}{t}", "w1_g1" if (b, t) == (1, 3) else None)
-                nc.vector.tensor_copy(ahead[b, t][:], ahead_all[b, t][:].indirect(pos2_t[:]))
+        def read_ahead(b, t, opened=None, tag=None):
+            full = held([P, S], F32, f"ahead_full{b}{t}", f"slot{4 * b + t}")
+            for half in range(2):
+                acc = opened[half] if opened else open_reading(w2_slice, b, t, half)
+                close_reading(acc, w2_slice, b, t, half, full)
+            ahead[b, t] = held([P, J], F32, f"ahead{b}{t}", tag)
+            nc.vector.tensor_copy(ahead[b, t][:], full[:].indirect(pos2_t[:]))
 
-        squares = [early[:, 0 : 4 * J].rearrange("p (t j) -> p t j", t=4), held([P, 4, J], F32, "squares1")[:]]
+        squares = {1: held([P, 4, J], F32, "squares1")[:]}
         logs = held([P, J, 4], F32, "logs")
+        behind_full = {}
 
-        def behind_all(b, t):
-            window = held([P, S], F32, f"behind_all{b}{t}", f"win{(0, 1, 3, 4, 8, 0, 1, 3)[4 * b + t]}")
-            cols = slice(128 * t, 128 * (t + 1))
-            for h in range(2):
-                first_half(window, h, lambda a: w1_c[a, b][:, cols], lambda a: w1_s[a, b][:, cols])
-            return window
+        def read_behind(b, t):
+            slot = BEHIND_SLOTS[(4 * b + t) % len(BEHIND_SLOTS)]
+            behind_full[b, t] = held([P, S], F32, f"behind_full{b}{t}", f"slot{slot}")
+            for half in range(2):
+                close_reading(open_reading(w1_slice, b, t, half), w1_slice, b, t, half, behind_full[b, t])
 
-        def contrast(window, b, t, c0, c1):
-            diff = squares[b][:, t, c0:c1]
+        def contrast(b, t, j0, j1):
+            diff = squares[b][:, t, j0:j1]
             nc.vector.tensor_tensor(
-                diff, window[:].indirect(pos1_t[:, c0 // 16 : c1 // 16]), ahead[b, t][:, c0:c1], ALU.subtract
+                diff, behind_full[b, t][:].indirect(pos1_t[:, j0 // 16 : j1 // 16]), ahead[b, t][:, j0:j1],
+                ALU.subtract,
             )
-            nc.scalar.activation(diff, diff, ACT.Square)
+            nc.scalar.activation(diff, diff, ACT.Square, bias=zero[:])
 
-        def log_h(b, c0, c1):
+        def log_h(b, j0, j1):
             nc.scalar.activation(
-                logs[:, c0:c1, :], squares[b][:, :, c0:c1].rearrange("p t j -> p j t"), ACT.Ln, bias=1.0
+                logs[:, j0:j1, :], squares[b][:, :, j0:j1].rearrange("p t j -> p j t"), ACT.Ln, bias=1.0
             )
 
         h_c = [held([P, J], U32, f"h_c{b}") for b in range(2)]
         h_s = [held([P, J], U8, f"h_s{b}") for b in range(2)]
         h_g = [held([P, 4 * J], BF16, f"h_g{b}") for b in range(2)]
 
-        def gain_h(b, c0, c1):
+        def gain_h(b, j0, j1):
             nc.vector.tensor_tensor(
-                h_g[b][:, 4 * c0 : 4 * c1].rearrange("p (j t) -> p j t", t=4),
-                logs[:, c0:c1, :],
-                gain_t[:, b : b + 1, :].to_broadcast([P, c1 - c0, 4]),
+                h_g[b][:, 4 * j0 : 4 * j1].rearrange("p (j t) -> p j t", t=4),
+                logs[:, j0:j1, :],
+                gain_t[:, b : b + 1, :].to_broadcast([P, j1 - j0, 4]),
                 ALU.mult,
             )
 
-        def quant_h(b, c0, c1):
+        def quantise_h(b, j0, j1):
             nc.vector.quantize_mx(
-                out=h_c[b][:, c0:c1].bitcast(FP8X4), scales=h_s[b][:, c0:c1], in_=h_g[b][:, 4 * c0 : 4 * c1]
+                out=h_c[b][:, j0:j1].bitcast(FP8X4), scales=h_s[b][:, j0:j1], in_=h_g[b][:, 4 * j0 : 4 * j1]
             )
 
-        opened = {}
-        for t, h in OPEN:
-            opened[t, h] = psum.tile([P, 512], F32, name="acc")
-            first_pass(opened[t, h], 0, h, w2_c[0][:, 0, 128 * t : 128 * (t + 1)], planes[:, 0, S + 128 * t : S + 128 * (t + 1)])
-        for t in range(4):
-            for h in range(2):
-                ahead_half(0, t, h, opened.get((t, h)))
-        for a, b in ((0, 0), (1, 0), (0, 1)):
-            cast_w1(a, b)
-        quant_w1(0, 0, "win2")
-        for h in range(2):
-            ahead_half(1, 0, h)
-        for h in range(2):
-            ahead_half(1, 1, h)
-        quant_w1(1, 0, "win5")
-        for t in range(2, 4):
-            for h in range(2):
-                ahead_half(1, t, h)
-        cast_w1(1, 1)
-        quant_w1(1, 1, "win6")
+        read_ahead(0, 0, opened=[open_reading(w2_slice, 0, 0, half) for half in range(2)])
+        for t in range(1, 4):
+            read_ahead(0, t)
+        for a in range(2):
+            round_w1_on_gpsimd(a, 0)
+        quantise_w1(0, 0, "slot2")
+        for t in range(2):
+            read_ahead(1, t)
+        quantise_w1(1, 0, "slot5")
+        read_ahead(1, 2)
+        read_ahead(1, 3, tag="w1_g1")
+        work = held([P, 5 * J], F32, "work", "slot6")
+        squares[0] = work[:, 0 : 4 * J].rearrange("p (t j) -> p t j", t=4)
+        for a in range(2):
+            w1_g[a, 1] = work[:, J + 2 * PASS * a : J + 2 * PASS * (a + 1)].bitcast(BF16)
+        for a in range(2):
+            round_w1_on_vector(a, 1)
+        quantise_w1(0, 1, "slot7")
 
-        behind = {0: behind_all(0, 0), 1: behind_all(0, 1)}
+        read_behind(0, 0)
+        read_behind(0, 1)
         for t in range(4):
-            behind[t + 2] = behind_all((t + 2) // 4, (t + 2) % 4)
-            contrast(behind[t], 0, t, 0, J)
+            read_behind(*divmod(t + 2, 4))
+            contrast(0, t, 0, J)
             if t == 0:
-                quant_w1(0, 1, "win7")
-        log_h(0, 0, 256)
-        behind[6] = behind_all(1, 2)
-        contrast(behind[4], 1, 0, 0, J)
-        log_h(0, 256, J)
-        gain_h(0, 0, 256)
-        behind[7] = behind_all(1, 3)
-        contrast(behind[5], 1, 1, 0, J)
-        gain_h(0, 256, J)
-        contrast(behind[6], 1, 2, 0, J)
-        quant_h(0, 0, J)
+                quantise_w1(1, 1)
+        log_h(0, 0, J // 2)
+        read_behind(1, 2)
+        contrast(1, 0, 0, J)
+        log_h(0, J // 2, J)
+        gain_h(0, 0, J // 2)
+        read_behind(1, 3)
+        contrast(1, 1, 0, J)
+        gain_h(0, J // 2, J)
+        contrast(1, 2, 0, J)
+        quantise_h(0, 0, J)
 
         y = held([P, 4, J], F32, "y")
         y_g = held([P, 4 * J], BF16, "y_g")
         y_c = held([P, J], U32, "y_c")
         y_s = held([P, J], U8, "y_s")
         out_rows = out_0.rearrange("(p t) j -> p t j", t=4)
-        out_words = out_1[0].rearrange("p m i -> p (m i)").bitcast(I32)
+        out_words = out_1[0].rearrange("p j i -> p (j i)").bitcast(I32)
+        chunks = J // CHUNK
+        forecast_sums = {}
 
-        sums = {}
-
-        def third(c):
-            cols = slice(128 * c, 128 * (c + 1))
-            acc = psum.tile([P, 512], F32, name="acc")
+        def forecast(c):
+            cols = slice(CHUNK * c, CHUNK * (c + 1))
+            forecast_sums[c] = psum.tile([P, PASS], F32, name="acc")
             for t in range(4):
+                first = S + H + P * t
                 for b in range(2):
                     nc.tensor.matmul_mx(
-                        out=acc[:, 128 * t : 128 * (t + 1)],
-                        lhsT=w3_c[:, b, 128 * t : 128 * (t + 1)].bitcast(FP4X4),
-                        lhsT_scale=planes[:, b, S + H + 128 * t : S + H + 128 * (t + 1)],
+                        out=forecast_sums[c][:, CHUNK * t : CHUNK * (t + 1)],
+                        lhsT=w3_c[:, b, P * t : P * (t + 1)].bitcast(FP4X4),
+                        lhsT_scale=planes[:, b, first : first + P],
                         rhs=h_c[b][:, cols].bitcast(FP8X4), rhs_scale=h_s[b][:, cols],
                         start=(b == 0), stop=(b == 1),
                     )
-            sums[c] = acc
 
-        def store_y(c):
-            cols = slice(128 * c, 128 * (c + 1))
-            nc.scalar.copy(y[:, :, cols], sums[c][:].rearrange("p (t j) -> p t j", t=4))
-            nc.sync.dma_start(out_rows[:, :, cols], y[:, :, cols])
-
-        def round_sums(c):
-            nc.scalar.copy(
-                y_g[:, 512 * c : 512 * (c + 1)].rearrange("p (j t) -> p j t", t=4),
-                sums[c][:].rearrange("p (t j) -> p j t", t=4),
-            )
-
-        def round_y(c):
-            nc.vector.tensor_copy(
-                y_g[:, 512 * c : 512 * (c + 1)].rearrange("p (u i t) -> p u t i", t=4, i=4),
-                y[:, :, 128 * c : 128 * (c + 1)].rearrange("p t (u i) -> p u t i", i=4),
-            )
-
-        def quant_y(c, n=1):
-            cols = slice(128 * c, 128 * (c + n))
-            nc.vector.quantize_mx(
-                out=y_c[:, cols].bitcast(FP8X4), scales=y_s[:, cols], in_=y_g[:, 512 * c : 512 * (c + n)]
-            )
-
-        def store_words(c0, c1):
-            nc.sync.dma_start(out_words[:, c0:c1], y_c[:, c0:c1].bitcast(I32))
-
-        for c in range(4):
-            contrast(behind[7], 1, 3, 128 * c, 128 * (c + 1))
-            log_h(1, 128 * c, 128 * (c + 1))
-        for c in range(5):
-            if c < 4:
-                gain_h(1, 128 * c, 128 * (c + 1))
+        for c in range(chunks):
+            contrast(1, 3, CHUNK * c, CHUNK * (c + 1))
+            log_h(1, CHUNK * c, CHUNK * (c + 1))
+        for c in range(chunks + 1):
+            if c < chunks:
+                gain_h(1, CHUNK * c, CHUNK * (c + 1))
             if c > 0:
-                quant_h(1, 128 * (c - 1), 128 * c)
-                third(c - 1)
-        for c in range(4):
-            store_y(c)
-            round_y(c)
+                quantise_h(1, CHUNK * (c - 1), CHUNK * c)
+                forecast(c - 1)
+        for c in range(chunks):
+            cols = slice(CHUNK * c, CHUNK * (c + 1))
+            nc.scalar.copy(y[:, :, cols], forecast_sums[c][:].rearrange("p (t j) -> p t j", t=4))
+            nc.sync.dma_start(out_rows[:, :, cols], y[:, :, cols])
+            nc.vector.tensor_copy(
+                y_g[:, 4 * CHUNK * c : 4 * CHUNK * (c + 1)].rearrange("p (u e t) -> p u t e", t=4, e=4),
+                y[:, :, cols].rearrange("p t (u e) -> p u t e", e=4),
+            )
             if c % 2:
-                quant_y(c - 1, 2)
-                store_words(128 * (c - 1), 128 * (c + 1))
-        for q in range(4):
-            eng = nc.scalar if q % 2 else nc.sync
-            eng.dma_start(out_2[0, 4 * q : 4 * q + 4, :].bitcast(I32), y_s[32 * q : 32 * q + 4, :].bitcast(I32))
+                pair = slice(CHUNK * (c - 1), CHUNK * (c + 1))
+                nc.vector.quantize_mx(
+                    out=y_c[:, pair].bitcast(FP8X4), scales=y_s[:, pair],
+                    in_=y_g[:, 4 * CHUNK * (c - 1) : 4 * CHUNK * (c + 1)],
+                )
+                nc.sync.dma_start(out_words[:, pair], y_c[:, pair].bitcast(I32))
+        for quad in range(4):
+            queue = nc.scalar if quad % 2 else nc.sync
+            queue.dma_start(
+                out_2[0, 4 * quad : 4 * quad + 4, :].bitcast(I32), y_s[32 * quad : 32 * quad + 4, :].bitcast(I32)
+            )

from contextlib import ExitStack

import concourse.mybir as mybir

K, H, N, T, S, J = 1024, 1024, 512, 4096, 1024, 512
P = 128
PASS = 512
CHUNK = 128
TOP = 96
FLOPS = 2 * (2 * K * H * S + H * N * J)

F32 = mybir.dt.float32
BF16 = mybir.dt.bfloat16
I32 = mybir.dt.int32
U32 = mybir.dt.uint32
U16 = mybir.dt.uint16
U8 = mybir.dt.uint8
FP8X4 = mybir.dt.float8_e4m3fn_x4
FP4X4 = mybir.dt.float4_e2m1fn_x4
ACT = mybir.ActivationFunctionType
ALU = mybir.AluOpType

BEHIND_SLOTS = (0, 1, 3, 4, 8)


def tile_list_ring_contrast_forecast_kernel(
    tc, tab_words, tab_scales, offs, pos1, pos2, w1, w2_words, w2_scales, gain, w3_words, w3_scales,
    out_0, out_1, out_2,
):
    nc = tc.nc
    with ExitStack() as ctx:
        lists = ctx.enter_context(tc.tile_pool(name="lists", bufs=1))
        keep = ctx.enter_context(tc.tile_pool(name="keep", bufs=1))
        psum = ctx.enter_context(tc.psum_pool(name="psum", bufs=8))

        def held(shape, dtype, name, tag=None):
            return keep.tile(shape, dtype, name=name, tag=tag or name, align_bytes=64)

        offs_t = lists.tile([P, S // 16], U16, name="offs_t")
        pos1_t = lists.tile([P, J // 16], U16, name="pos1_t")
        pos2_t = lists.tile([P, J // 16], U16, name="pos2_t")

        tab_s = held([P, T], U8, "tab_s")
        w_s_raw = held([P, H + N], U8, "w_s_raw")
        planes = held([P, 2, S + H + N], U8, "planes")
        nc.vector.memset(w_s_raw[0:TOP, :].bitcast(I32), 0)
        nc.vector.memset(tab_s[0:TOP, :].bitcast(I32), 0)
        nc.gpsimd.memset(planes[:].bitcast(I32), 0)
        one = held([P, 1], F32, "one")
        nc.gpsimd.memset(one[:], 1.0)
        zero = held([P, 1], F32, "zero")
        nc.scalar.activation(zero[:], one[:], ACT.Ln)

        nc.sync.dma_start(offs_t[:], offs)
        nc.sync.dma_start(w_s_raw[TOP:P, 0:H].bitcast(I32), w2_scales.bitcast(I32).rearrange("a q r -> q a r"))
        nc.sync.dma_start(w_s_raw[TOP:P, H : H + N].bitcast(I32), w3_scales.bitcast(I32).rearrange("b q n -> q b n"))
        nc.sync.dma_start(tab_s[TOP:P, :].bitcast(I32), tab_scales.bitcast(I32).rearrange("a q s -> q a s"))
        tab_w = [held([P, T], U16, f"tab_w{a}") for a in range(2)]
        nc.sync.dma_start(tab_w[0][:].bitcast(I32), tab_words[0].bitcast(I32))
        w2_raw = [held([P, 2, PASS], I32, f"w2_raw{b}") for b in range(2)]
        w2_src = w2_words.rearrange("a p r i -> p a (r i)").bitcast(I32)
        for b in range(2):
            nc.sync.dma_start(w2_raw[b][:], w2_src[:, :, PASS * b : PASS * (b + 1)])
        nc.sync.dma_start(pos2_t[:], pos2)
        nc.sync.dma_start(pos1_t[:], pos1)
        nc.sync.dma_start(tab_w[1][:].bitcast(I32), tab_words[1].bitcast(I32))
        w3_raw = held([P, 2, N], U16, "w3_raw")
        nc.sync.dma_start(w3_raw[:].bitcast(I32), w3_words.bitcast(I32).rearrange("b p n -> p b n"))

        rows = held([P, S + H + N], U8, "rows")
        nc.vector.tensor_copy(
            rows[:, S:].rearrange("p (x t u e) -> p u x t e", t=4, u=8, e=16),
            w_s_raw[:].rearrange("p (x u e t) -> p u x t e", t=4, u=8, e=16),
        )
        gain_t = held([P, 2, 4], F32, "gain_t", "w_s_raw")
        nc.sync.dma_start(gain_t[:], gain.rearrange("(b p t) -> p b t", b=2, t=4))
        picked_s = held([P, S], U8, "picked_s")
        nc.vector.tensor_copy(picked_s[:], tab_s[:].indirect(offs_t[:]))
        nc.vector.tensor_copy(rows[:, 0:S].bitcast(I32), picked_s[:].bitcast(I32))
        for quad in range(4):
            nc.scalar.dma_start(
                planes[32 * quad : 32 * quad + 4].bitcast(I32),
                rows[TOP + 8 * quad : TOP + 8 * quad + 8, :].bitcast(I32),
            )
        w1_all = held([P, 4 * 4 * PASS], F32, "w1_all", "rows")
        w1_raw = {}
        for b in range(2):
            for a in range(2):
                first = 4 * PASS * (2 * b + a)
                w1_raw[a, b] = w1_all[:, first : first + 4 * PASS].rearrange("p (i r) -> p i r", i=4)
                nc.sync.dma_start(
                    w1_raw[a, b],
                    w1[PASS * a : PASS * (a + 1), PASS * b : PASS * (b + 1)].rearrange("(p i) r -> p i r", i=4),
                )

        picked_w = [[held([P, PASS], U16, f"picked_w{a}{half}") for half in range(2)] for a in range(2)]

        def gather_words(a, half):
            entries = offs_t[:, PASS // 16 * half : PASS // 16 * (half + 1)]
            nc.vector.tensor_copy(picked_w[a][half][:], tab_w[a][:].indirect(entries))

        w2_c = {}

        def deal_w2(b, tag):
            w2_c[b] = held([P, 2, PASS], I32, f"w2_c{b}", tag)
            nc.vector.tensor_copy(
                w2_c[b][:].rearrange("p a (t u e) -> p a u t e", t=4, e=4),
                w2_raw[b][:].rearrange("p a (u e t) -> p a u t e", t=4, e=4),
            )

        gather_words(0, 0)
        deal_w2(0, "w2_c0")
        gather_words(0, 1)
        deal_w2(1, "tab_w0")
        gather_words(1, 0)
        gather_words(1, 1)
        w3_c = held([P, 2, N], U16, "w3_c", "tab_w1")
        nc.vector.tensor_copy(
            w3_c[:].rearrange("p b (t u e) -> p b u t e", t=4, e=8),
            w3_raw[:].rearrange("p b (u e t) -> p b u t e", t=4, e=8),
        )

        w1_c = {}
        w1_s = {}
        w1_g = {(a, 0): held([P, 4 * PASS], BF16, f"w1_g{a}")[:] for a in range(2)}

        def w1_views(a, b):
            return (
                w1_g[a, b].rearrange("p (t m i) -> p m t i", t=4, i=4),
                w1_raw[a, b].rearrange("p i (m t) -> p m t i", t=4),
            )

        def round_w1_on_gpsimd(a, b):
            dst, src = w1_views(a, b)
            for piece in range(4):
                part = slice(32 * piece, 32 * (piece + 1))
                nc.gpsimd.tensor_scalar(dst[:, part], src[:, part], 1.0, 0.0, ALU.mult, ALU.add)

        def round_w1_on_vector(a, b):
            dst, src = w1_views(a, b)
            nc.vector.tensor_copy(dst, src)

        def quantise_w1(a, b, tag=None):
            w1_c[a, b] = held([P, PASS], U32, f"w1_c{a}{b}", tag)
            w1_s[a, b] = held([P, PASS], U8, f"w1_s{a}{b}")
            nc.vector.quantize_mx(out=w1_c[a, b][:].bitcast(FP8X4), scales=w1_s[a, b][:], in_=w1_g[a, b])

        def w1_slice(a, b, t):
            return w1_c[a, b][:, P * t : P * (t + 1)], w1_s[a, b][:, P * t : P * (t + 1)]

        def w2_slice(a, b, t):
            first = S + PASS * b + P * t
            return w2_c[b][:, a, P * t : P * (t + 1)], planes[:, a, first : first + P]

        def reading_pass(acc, weight_slice, a, b, t, half):
            codes, scales = weight_slice(a, b, t)
            nc.tensor.matmul_mx(
                out=acc[:], lhsT=codes.bitcast(FP8X4), lhsT_scale=scales,
                rhs=picked_w[a][half][:].bitcast(FP4X4), rhs_scale=planes[:, a, PASS * half : PASS * (half + 1)],
                start=(a == 0), stop=(a == 1),
            )

        def open_reading(weight_slice, b, t, half):
            acc = psum.tile([P, PASS], F32, name="acc")
            reading_pass(acc, weight_slice, 0, b, t, half)
            return acc

        def close_reading(acc, weight_slice, b, t, half, full):
            reading_pass(acc, weight_slice, 1, b, t, half)
            nc.scalar.copy(full[:, PASS * half : PASS * (half + 1)], acc[:])

        ahead = {}

        def read_ahead(b, t, opened=None, tag=None):
            full = held([P, S], F32, f"ahead_full{b}{t}", f"slot{4 * b + t}")
            for half in range(2):
                acc = opened[half] if opened else open_reading(w2_slice, b, t, half)
                close_reading(acc, w2_slice, b, t, half, full)
            ahead[b, t] = held([P, J], F32, f"ahead{b}{t}", tag)
            nc.vector.tensor_copy(ahead[b, t][:], full[:].indirect(pos2_t[:]))

        squares = {1: held([P, 4, J], F32, "squares1")[:]}
        logs = held([P, J, 4], F32, "logs")
        behind_full = {}

        def read_behind(b, t):
            slot = BEHIND_SLOTS[(4 * b + t) % len(BEHIND_SLOTS)]
            behind_full[b, t] = held([P, S], F32, f"behind_full{b}{t}", f"slot{slot}")
            for half in range(2):
                close_reading(open_reading(w1_slice, b, t, half), w1_slice, b, t, half, behind_full[b, t])

        def contrast(b, t, j0, j1):
            diff = squares[b][:, t, j0:j1]
            nc.vector.tensor_tensor(
                diff, behind_full[b, t][:].indirect(pos1_t[:, j0 // 16 : j1 // 16]), ahead[b, t][:, j0:j1],
                ALU.subtract,
            )
            nc.scalar.activation(diff, diff, ACT.Square, bias=zero[:])

        def log_h(b, j0, j1):
            nc.scalar.activation(
                logs[:, j0:j1, :], squares[b][:, :, j0:j1].rearrange("p t j -> p j t"), ACT.Ln, bias=1.0
            )

        h_c = [held([P, J], U32, f"h_c{b}") for b in range(2)]
        h_s = [held([P, J], U8, f"h_s{b}") for b in range(2)]
        h_g = [held([P, 4 * J], BF16, f"h_g{b}") for b in range(2)]

        def gain_h(b, j0, j1):
            nc.vector.tensor_tensor(
                h_g[b][:, 4 * j0 : 4 * j1].rearrange("p (j t) -> p j t", t=4),
                logs[:, j0:j1, :],
                gain_t[:, b : b + 1, :].to_broadcast([P, j1 - j0, 4]),
                ALU.mult,
            )

        def quantise_h(b, j0, j1):
            nc.vector.quantize_mx(
                out=h_c[b][:, j0:j1].bitcast(FP8X4), scales=h_s[b][:, j0:j1], in_=h_g[b][:, 4 * j0 : 4 * j1]
            )

        read_ahead(0, 0, opened=[open_reading(w2_slice, 0, 0, half) for half in range(2)])
        for t in range(1, 4):
            read_ahead(0, t)
        for a in range(2):
            round_w1_on_gpsimd(a, 0)
        quantise_w1(0, 0, "slot2")
        for t in range(2):
            read_ahead(1, t)
        quantise_w1(1, 0, "slot5")
        read_ahead(1, 2)
        read_ahead(1, 3, tag="w1_g1")
        work = held([P, 5 * J], F32, "work", "slot6")
        squares[0] = work[:, 0 : 4 * J].rearrange("p (t j) -> p t j", t=4)
        for a in range(2):
            w1_g[a, 1] = work[:, J + 2 * PASS * a : J + 2 * PASS * (a + 1)].bitcast(BF16)
        for a in range(2):
            round_w1_on_vector(a, 1)
        quantise_w1(0, 1, "slot7")

        read_behind(0, 0)
        read_behind(0, 1)
        for t in range(4):
            read_behind(*divmod(t + 2, 4))
            contrast(0, t, 0, J)
            if t == 0:
                quantise_w1(1, 1)
        log_h(0, 0, J // 2)
        read_behind(1, 2)
        contrast(1, 0, 0, J)
        log_h(0, J // 2, J)
        gain_h(0, 0, J // 2)
        read_behind(1, 3)
        contrast(1, 1, 0, J)
        gain_h(0, J // 2, J)
        contrast(1, 2, 0, J)
        quantise_h(0, 0, J)

        y = held([P, 4, J], F32, "y")
        y_g = held([P, 4 * J], BF16, "y_g")
        y_c = held([P, J], U32, "y_c")
        y_s = held([P, J], U8, "y_s")
        out_rows = out_0.rearrange("(p t) j -> p t j", t=4)
        out_words = out_1[0].rearrange("p j i -> p (j i)").bitcast(I32)
        chunks = J // CHUNK
        forecast_sums = {}

        def forecast(c):
            cols = slice(CHUNK * c, CHUNK * (c + 1))
            forecast_sums[c] = psum.tile([P, PASS], F32, name="acc")
            for t in range(4):
                first = S + H + P * t
                for b in range(2):
                    nc.tensor.matmul_mx(
                        out=forecast_sums[c][:, CHUNK * t : CHUNK * (t + 1)],
                        lhsT=w3_c[:, b, P * t : P * (t + 1)].bitcast(FP4X4),
                        lhsT_scale=planes[:, b, first : first + P],
                        rhs=h_c[b][:, cols].bitcast(FP8X4), rhs_scale=h_s[b][:, cols],
                        start=(b == 0), stop=(b == 1),
                    )

        for c in range(chunks):
            contrast(1, 3, CHUNK * c, CHUNK * (c + 1))
            log_h(1, CHUNK * c, CHUNK * (c + 1))
        for c in range(chunks + 1):
            if c < chunks:
                gain_h(1, CHUNK * c, CHUNK * (c + 1))
            if c > 0:
                quantise_h(1, CHUNK * (c - 1), CHUNK * c)
                forecast(c - 1)
        for c in range(chunks):
            cols = slice(CHUNK * c, CHUNK * (c + 1))
            nc.scalar.copy(y[:, :, cols], forecast_sums[c][:].rearrange("p (t j) -> p t j", t=4))
            nc.sync.dma_start(out_rows[:, :, cols], y[:, :, cols])
            nc.vector.tensor_copy(
                y_g[:, 4 * CHUNK * c : 4 * CHUNK * (c + 1)].rearrange("p (u e t) -> p u t e", t=4, e=4),
                y[:, :, cols].rearrange("p t (u e) -> p u t e", e=4),
            )
            if c % 2:
                pair = slice(CHUNK * (c - 1), CHUNK * (c + 1))
                nc.vector.quantize_mx(
                    out=y_c[:, pair].bitcast(FP8X4), scales=y_s[:, pair],
                    in_=y_g[:, 4 * CHUNK * (c - 1) : 4 * CHUNK * (c + 1)],
                )
                nc.sync.dma_start(out_words[:, pair], y_c[:, pair].bitcast(I32))
        for quad in range(4):
            queue = nc.scalar if quad % 2 else nc.sync
            queue.dma_start(
                out_2[0, 4 * quad : 4 * quad + 4, :].bitcast(I32), y_s[32 * quad : 32 * quad + 4, :].bitcast(I32)
            )
